import numpy as np
import ml_dtypes


def mxq(x, axis, fmt="e4m3"):
    dtype, down = {"e4m3": (ml_dtypes.float8_e4m3fn, 7), "e5m2": (ml_dtypes.float8_e5m2, 14)}[fmt]
    v = np.moveaxis(np.asarray(x, np.float32).astype(ml_dtypes.bfloat16).astype(np.float64), axis, -1)
    blocks = v.reshape(v.shape[:-1] + (-1, 32))
    amax = np.abs(blocks).max(-1, keepdims=True)
    byte = np.maximum(np.where(amax > 0, np.frexp(amax)[1] - 1 + 127, 0) - down, 1)
    scale = np.exp2(byte - 127.0)
    codes = (blocks / scale).astype(np.float32).astype(dtype).astype(np.float64)
    return np.moveaxis((codes * scale).reshape(v.shape), -1, axis)


WIDE = False


def mx_kscale(k):
    if not WIDE:
        return np.ones(k)
    levels = np.array([18, -18])
    if k % 512:
        return np.exp2(np.random.permutation(np.resize(levels, k // 32))).repeat(32)
    a = np.empty((k // 512, 16))
    for p in range(k // 512):
        a[p, :8] = np.random.permutation(np.resize(levels, 8))
        for g in range(8):
            far = levels[np.abs(levels - a[p, g]) >= 10]
            a[p, g + 8] = far[np.random.randint(len(far))]
    return np.exp2(a.ravel()).repeat(32)


def f64(x):
    return np.asarray(x).astype(np.float64)


def striped(idx):
    return np.tile(np.asarray(idx).reshape(-1, 16).T, (8, 1)).astype(np.uint16)


def unstriped(offs):
    return offs[:16].T.reshape(-1).astype(np.int64)


B, N, T, D, R = 1, 512, 2048, 512, 512
PAGE = 32


def setup_inputs():
    n = np.random.standard_normal
    pages = np.random.permutation(T // PAGE)[:B * N // PAGE]
    idx = (pages[:, None] * PAGE + np.arange(PAGE)[None, :]).reshape(-1)
    s = mx_kscale(D)[:, None]
    z = mx_kscale(R)[:, None]
    x = n((B, D, R))
    return {
        "xT": (x * s).astype(np.float32),
        "wT": (n((D, T)) * (1.00 / np.sqrt(D)) / s).astype(np.float32),
        "vT": (n((D, T)) / np.sqrt(D) / s).astype(np.float32),
        "y": n((B, R, N)).astype(np.float32),
        "wt": (np.random.uniform(0.5, 1.5, (B, R, 1)) * 1.0 / np.sqrt(R) * z).astype(np.float32),
        "xm": (x.transpose(0, 2, 1) / z).astype(np.float32),
        "offs": striped(idx),
    }


def reference(xT, wT, vT, y, wt, xm, offs):
    idx = unstriped(offs)
    pick = lambda x: x[:, idx].reshape(x.shape[0], B, N).transpose(1, 0, 2)
    xq = mxq(f64(xT), 1, "e4m3").transpose(0, 2, 1)
    a = xq @ mxq(pick(f64(wT)), 1, "e4m3")
    av = xq @ mxq(pick(f64(vT)), 1, "e4m3")
    q = np.tanh(a - f64(y))
    g = f64(wt) * (1.0 - q * q) * av
    dw = mxq(f64(xm), 1, "e4m3").transpose(0, 2, 1) @ mxq(g, 1, "e5m2")
    gw = np.zeros((D, T))
    gw[:, idx] = dw.transpose(1, 0, 2).reshape(D, B * N)
    return gw

@@ -1,0 +1,185 @@
+from contextlib import ExitStack
+
+import concourse.mybir as mybir
+
+N, T, D, R = 512, 2048, 512, 512
+FLOPS = 3 * 2 * D * R * N
+
+F32 = mybir.dt.float32
+BF16 = mybir.dt.bfloat16
+U32 = mybir.dt.uint32
+U16 = mybir.dt.uint16
+U8 = mybir.dt.uint8
+E4M3 = mybir.dt.float8_e4m3fn_x4
+E5M2 = mybir.dt.float8_e5m2_x4
+ALU = mybir.AluOpType
+ACT = mybir.ActivationFunctionType
+
+P = 128
+PACK = 4
+Q = 128
+
+
+def tile_attend_ghv_lch_kernel(tc, xT, wT, vT, y, wt, xm, offs, out):
+    nc = tc.nc
+    with ExitStack() as ctx:
+        keep = ctx.enter_context(tc.tile_pool(name="keep", bufs=1))
+        psum = ctx.enter_context(tc.psum_pool(name="psum", bufs=1))
+
+        def sb(name, shape, dtype):
+            return keep.tile(shape, dtype, name=name, align_bytes=64)
+
+        offsets = keep.tile([P, N // 16], U16, name="offsets")
+        x_raw = sb("x_raw", [P, PACK, R], F32)
+        w_pl = [sb(f"w_pl{t}", [P, T], F32) for t in range(PACK)]
+        v_pl = [sb(f"v_pl{t}", [P, T], F32) for t in range(PACK)]
+        y_sb = sb("y_sb", [P, PACK, N], F32)
+        wt_sb = sb("wt_sb", [P, PACK], F32)
+        xm_head = sb("xm_head", [P, PACK, P], F32)
+        xm_rest = sb("xm_rest", [P, PACK, D - P], F32)
+
+        w_rows = wT.rearrange("(p t) c -> p t c", t=PACK)
+        v_rows = vT.rearrange("(p t) c -> p t c", t=PACK)
+        xm_rows = xm.rearrange("b (p t) d -> p (b t) d", t=PACK)
+        nc.sync.dma_start(out=x_raw[:], in_=xT.rearrange("b (p t) r -> p (b t) r", t=PACK))
+        nc.sync.dma_start(offsets[:], offs)
+        for t in range(PACK):
+            nc.sync.dma_start(out=w_pl[t][:], in_=w_rows[:, t, :])
+        nc.sync.dma_start(out=wt_sb[:], in_=wt.rearrange("b (p t) o -> p (b t o)", t=PACK))
+        nc.sync.dma_start(out=y_sb[:], in_=y.rearrange("b (p t) i -> p (b t) i", t=PACK))
+        for t in range(PACK):
+            nc.sync.dma_start(out=v_pl[t][:], in_=v_rows[:, t, :])
+        nc.sync.dma_start(out=xm_head[:], in_=xm_rows[:, :, 0:P])
+        nc.sync.dma_start(out=xm_rest[:], in_=xm_rows[:, :, P:D])
+
+        x_bf = sb("x_bf", [P, R * PACK], BF16)
+        x_codes = sb("x_codes", [P, R], U32)
+        x_scales = sb("x_scales", [P, R], U8)
+        nc.scalar.copy(
+            out=x_bf[:].rearrange("p (t m j) -> p m j t", t=PACK, j=PACK),
+            in_=x_raw[:].rearrange("p j (m t) -> p m j t", t=PACK),
+        )
+        nc.vector.quantize_mx(out=x_codes[:].bitcast(E4M3), scales=x_scales[:], in_=x_bf[:])
+
+        neg_wt = sb("neg_wt", [P, PACK], F32)
+        nc.vector.tensor_scalar(out=neg_wt[:], in0=wt_sb[:], scalar1=-1.0, scalar2=None, op0=ALU.mult)
+
+        def scores(name, codes, scales, n):
+            bank = psum.tile([P, PACK, Q], F32, name=name)
+            cols = slice(n * Q, (n + 1) * Q)
+            for t in range(PACK):
+                rows = slice(t * P, (t + 1) * P)
+                nc.tensor.matmul_mx(
+                    out=bank[:, t, :],
+                    lhsT=x_codes[:, rows].bitcast(E4M3),
+                    lhsT_scale=x_scales[:, rows],
+                    rhs=codes[:, cols].bitcast(E4M3),
+                    rhs_scale=scales[:, cols],
+                    start=True,
+                    stop=True,
+                )
+            return bank
+
+        w_bf = sb("w_bf", [P, N, PACK], BF16)
+        w_codes = sb("w_codes", [P, N], U32)
+        w_scales = sb("w_scales", [P, N], U8)
+        for t in range(PACK):
+            nc.vector.tensor_copy(w_bf[:, :, t], w_pl[t][:].indirect(offsets[:]))
+        nc.vector.quantize_mx(out=w_codes[:].bitcast(E4M3), scales=w_scales[:], in_=w_bf[:].rearrange("p n t -> p (n t)"))
+
+        z = sb("z", [P, N, PACK], F32)
+        q = sb("q", [P, N, PACK], F32)
+        q2 = sb("q2", [P, N, PACK], F32)
+        h = sb("h", [P, N, PACK], F32)
+        for n in range(PACK):
+            cols = slice(n * Q, (n + 1) * Q)
+            a = scores(f"bank{n}", w_codes, w_scales, n)
+            nc.vector.tensor_tensor(
+                out=z[:, cols, :],
+                in0=a[:].rearrange("p t i -> p i t"),
+                in1=y_sb[:, :, cols].rearrange("p t i -> p i t"),
+                op=ALU.subtract,
+            )
+            nc.scalar.activation(out=q[:, cols, :], in_=z[:, cols, :], func=ACT.Tanh)
+            nc.scalar.activation(out=q2[:, cols, :], in_=q[:, cols, :], func=ACT.Square)
+        for n in range(PACK):
+            cols = slice(n * Q, (n + 1) * Q)
+            nc.vector.scalar_tensor_tensor(
+                out=h[:, cols, :],
+                in0=q2[:, cols, :],
+                scalar=1.0,
+                in1=neg_wt[:].unsqueeze(1).to_broadcast([P, Q, PACK]),
+                op0=ALU.subtract,
+                op1=ALU.mult,
+            )
+
+        v_bf = sb("v_bf", [P, N, PACK], BF16)
+        v_codes = sb("v_codes", [P, N], U32)
+        v_scales = sb("v_scales", [P, N], U8)
+        for t in range(PACK - 1):
+            nc.vector.tensor_copy(v_bf[:, :, t], v_pl[t][:].indirect(offsets[:]))
+        for half in range(2):
+            cols = slice(half * N // 2, (half + 1) * N // 2)
+            nc.vector.tensor_copy(v_bf[:, cols, PACK - 1], v_pl[PACK - 1][:].indirect(offsets[:, half * 16 : (half + 1) * 16]))
+        for half in range(2):
+            cols = slice(half * N // 2, (half + 1) * N // 2)
+            nc.vector.quantize_mx(
+                out=v_codes[:, cols].bitcast(E4M3), scales=v_scales[:, cols], in_=v_bf[:, cols, :].rearrange("p n t -> p (n t)")
+            )
+
+        xm_bf = sb("xm_bf", [P, D, PACK], BF16)
+        xm_codes = sb("xm_codes", [P, D], U32)
+        xm_scales = sb("xm_scales", [P, D], U8)
+
+        def cast_xm(m):
+            src = xm_head[:] if m == 0 else xm_rest[:, :, (m - 1) * P : m * P]
+            nc.scalar.copy(
+                out=xm_bf[:, m * P : (m + 1) * P, :].rearrange("p (c i) t -> p c t i", i=4),
+                in_=src.rearrange("p t (c i) -> p c t i", i=4),
+            )
+
+        def quantize_xm(m):
+            cols = slice(m * P, (m + 1) * P)
+            nc.vector.quantize_mx(
+                out=xm_codes[:, cols].bitcast(E4M3), scales=xm_scales[:, cols], in_=xm_bf[:, cols, :].rearrange("p d t -> p (d t)")
+            )
+
+        cast_xm(0)
+        g_bf = sb("g_bf", [P, N, PACK], BF16)
+        g_codes = sb("g_codes", [P, N], U32)
+        g_scales = sb("g_scales", [P, N], U8)
+        for n in range(PACK):
+            cols = slice(n * Q, (n + 1) * Q)
+            av = scores(f"bank{PACK + n}", v_codes, v_scales, n)
+            nc.vector.tensor_tensor(out=g_bf[:, cols, :], in0=av[:].rearrange("p t i -> p i t"), in1=h[:, cols, :], op=ALU.mult)
+        quantize_xm(0)
+        nc.vector.quantize_mx(out=g_codes[:].bitcast(E5M2), scales=g_scales[:], in_=g_bf[:].rearrange("p n t -> p (n t)"))
+        for m in range(1, PACK):
+            cast_xm(m)
+
+        for m in range(D // P):
+            cols = slice(m * P, (m + 1) * P)
+            if m > 0:
+                quantize_xm(m)
+            dw = psum.tile([P, N], F32, name=f"bank{m}")
+            nc.tensor.matmul_mx(
+                out=dw[:],
+                lhsT=xm_codes[:, cols].bitcast(E4M3),
+                lhsT_scale=xm_scales[:, cols],
+                rhs=g_codes[:].bitcast(E5M2),
+                rhs_scale=g_scales[:],
+                start=True,
+                stop=True,
+            )
+            dense = sb(f"dense{m}", [P, N], F32)
+            wide = sb(f"wide{m}", [P, T], F32)
+            nc.vector.memset(wide[:], 0.0)
+            if m == 0:
+                for half in range(2):
+                    hc = slice(half * N // 2, (half + 1) * N // 2)
+                    nc.scalar.copy(out=dense[:, hc], in_=dw[:, hc])
+                    nc.vector.tensor_copy(wide[:].indirect(offsets[:, half * 16 : (half + 1) * 16]), dense[:, hc])
+            else:
+                nc.scalar.copy(out=dense[:], in_=dw[:])
+                nc.vector.tensor_copy(wide[:].indirect(offsets[:]), dense[:])
+            nc.sync.dma_start(out=out[cols, :], in_=wide[:])

@@ -55,9 +55,9 @@ def tile_attend_ghv_lch_kernel(tc, xT, wT, vT, y, wt, xm, offs, out):
         x_bf = sb("x_bf", [P, R * PACK], BF16)
         x_codes = sb("x_codes", [P, R], U32)
         x_scales = sb("x_scales", [P, R], U8)
-        nc.scalar.copy(
-            out=x_bf[:].rearrange("p (t m j) -> p m j t", t=PACK, j=PACK),
-            in_=x_raw[:].rearrange("p j (m t) -> p m j t", t=PACK),
+        nc.vector.tensor_copy(
+            out=x_bf[:].rearrange("p (t m j) -> p t m j", t=PACK, j=PACK),
+            in_=x_raw[:].rearrange("p j (m t) -> p t m j", t=PACK),
         )
         nc.vector.quantize_mx(out=x_codes[:].bitcast(E4M3), scales=x_scales[:], in_=x_bf[:])
 
@@ -80,12 +80,23 @@ def tile_attend_ghv_lch_kernel(tc, xT, wT, vT, y, wt, xm, offs, out):
                 )
             return bank
 
+        def interleave(copy, dst, src):
+            copy(out=dst.rearrange("p (c i) t -> p c t i", i=4), in_=src.rearrange("p t (c i) -> p c t i", i=4))
+
+        def quantize(codes, scales, src, cols, fmt):
+            nc.vector.quantize_mx(out=codes[:, cols].bitcast(fmt), scales=scales[:, cols], in_=src[:, cols, :].rearrange("p n t -> p (n t)"))
+
+        quarter = [slice(n * Q, (n + 1) * Q) for n in range(PACK)]
+        w_got = sb("w_got", [P, PACK, N], F32)
         w_bf = sb("w_bf", [P, N, PACK], BF16)
         w_codes = sb("w_codes", [P, N], U32)
         w_scales = sb("w_scales", [P, N], U8)
         for t in range(PACK):
-            nc.vector.tensor_copy(w_bf[:, :, t], w_pl[t][:].indirect(offsets[:]))
-        nc.vector.quantize_mx(out=w_codes[:].bitcast(E4M3), scales=w_scales[:], in_=w_bf[:].rearrange("p n t -> p (n t)"))
+            nc.vector.tensor_copy(w_got[:, t, :], w_pl[t][:].indirect(offsets[:]))
+        for n in range(PACK):
+            interleave(nc.vector.tensor_copy if n < 2 else nc.scalar.copy, w_bf[:, quarter[n], :], w_got[:, :, quarter[n]])
+        for n in range(PACK):
+            quantize(w_codes, w_scales, w_bf, quarter[n], E4M3)
 
         z = sb("z", [P, N, PACK], F32)
         q = sb("q", [P, N, PACK], F32)
@@ -116,16 +127,27 @@ def tile_attend_ghv_lch_kernel(tc, xT, wT, vT, y, wt, xm, offs, out):
         v_bf = sb("v_bf", [P, N, PACK], BF16)
         v_codes = sb("v_codes", [P, N], U32)
         v_scales = sb("v_scales", [P, N], U8)
+        v_got = sb("v_got", [P, PACK, N], F32)
         for t in range(PACK - 1):
-            nc.vector.tensor_copy(v_bf[:, :, t], v_pl[t][:].indirect(offsets[:]))
-        for half in range(2):
+            nc.vector.tensor_copy(v_got[:, t, :], v_pl[t][:].indirect(offsets[:]))
+
+        def gather_last(half):
             cols = slice(half * N // 2, (half + 1) * N // 2)
-            nc.vector.tensor_copy(v_bf[:, cols, PACK - 1], v_pl[PACK - 1][:].indirect(offsets[:, half * 16 : (half + 1) * 16]))
-        for half in range(2):
-            cols = slice(half * N // 2, (half + 1) * N // 2)
-            nc.vector.quantize_mx(
-                out=v_codes[:, cols].bitcast(E4M3), scales=v_scales[:, cols], in_=v_bf[:, cols, :].rearrange("p n t -> p (n t)")
-            )
+            nc.vector.tensor_copy(v_got[:, PACK - 1, cols], v_pl[PACK - 1][:].indirect(offsets[:, half * 16 : (half + 1) * 16]))
+
+        def interleave_v(copy, n):
+            interleave(copy, v_bf[:, quarter[n], :], v_got[:, :, quarter[n]])
+
+        gather_last(0)
+        interleave_v(nc.vector.tensor_copy, 0)
+        interleave_v(nc.scalar.copy, 1)
+        gather_last(1)
+        interleave_v(nc.scalar.copy, 2)
+        quantize(v_codes, v_scales, v_bf, quarter[0], E4M3)
+        quantize(v_codes, v_scales, v_bf, quarter[1], E4M3)
+        interleave_v(nc.vector.tensor_copy, 3)
+        quantize(v_codes, v_scales, v_bf, quarter[2], E4M3)
+        quantize(v_codes, v_scales, v_bf, quarter[3], E4M3)
 
         xm_bf = sb("xm_bf", [P, D, PACK], BF16)
         xm_codes = sb("xm_codes", [P, D], U32)
@@ -173,7 +195,7 @@ def tile_attend_ghv_lch_kernel(tc, xT, wT, vT, y, wt, xm, offs, out):
             )
             dense = sb(f"dense{m}", [P, N], F32)
             wide = sb(f"wide{m}", [P, T], F32)
-            nc.vector.memset(wide[:], 0.0)
+            nc.vector.memset(wide[:].bitcast(mybir.dt.int32), 0)
             if m == 0:
                 for half in range(2):
                     hc = slice(half * N // 2, (half + 1) * N // 2)

@@ -31,31 +31,35 @@ def tile_attend_ghv_lch_kernel(tc, xT, wT, vT, y, wt, xm, offs, out):
 
         offsets = keep.tile([P, N // 16], U16, name="offsets")
         x_raw = sb("x_raw", [P, PACK, R], F32)
-        w_pl = [sb(f"w_pl{t}", [P, T], F32) for t in range(PACK)]
-        v_pl = [sb(f"v_pl{t}", [P, T], F32) for t in range(PACK)]
+        w_pair = sb("w_pair", [P, 2, T], F32)
+        w_late = [sb(f"w_late{u}", [P, T], F32) for u in range(2)]
+        v_pair = sb("v_pair", [P, 2, T], F32)
+        v_late = [sb(f"v_late{u}", [P, T], F32) for u in range(2)]
+        w_pl = [w_pair[:, 0, :], w_pair[:, 1, :], w_late[0][:], w_late[1][:]]
+        v_pl = [v_pair[:, 0, :], v_pair[:, 1, :], v_late[0][:], v_late[1][:]]
         y_sb = sb("y_sb", [P, PACK, N], F32)
         wt_sb = sb("wt_sb", [P, PACK], F32)
-        xm_head = sb("xm_head", [P, PACK, P], F32)
-        xm_rest = sb("xm_rest", [P, PACK, D - P], F32)
+        xm_raw = sb("xm_raw", [P, PACK, D], F32)
 
         w_rows = wT.rearrange("(p t) c -> p t c", t=PACK)
         v_rows = vT.rearrange("(p t) c -> p t c", t=PACK)
         xm_rows = xm.rearrange("b (p t) d -> p (b t) d", t=PACK)
         nc.sync.dma_start(out=x_raw[:], in_=xT.rearrange("b (p t) r -> p (b t) r", t=PACK))
         nc.sync.dma_start(offsets[:], offs)
-        for t in range(PACK):
-            nc.sync.dma_start(out=w_pl[t][:], in_=w_rows[:, t, :])
+        nc.sync.dma_start(out=w_pair[:], in_=w_rows[:, 0:2, :])
+        for u in range(2):
+            nc.sync.dma_start(out=w_late[u][:], in_=w_rows[:, 2 + u, :])
         nc.sync.dma_start(out=wt_sb[:], in_=wt.rearrange("b (p t) o -> p (b t o)", t=PACK))
         nc.sync.dma_start(out=y_sb[:], in_=y.rearrange("b (p t) i -> p (b t) i", t=PACK))
-        for t in range(PACK):
-            nc.sync.dma_start(out=v_pl[t][:], in_=v_rows[:, t, :])
-        nc.sync.dma_start(out=xm_head[:], in_=xm_rows[:, :, 0:P])
-        nc.sync.dma_start(out=xm_rest[:], in_=xm_rows[:, :, P:D])
+        nc.sync.dma_start(out=v_pair[:], in_=v_rows[:, 0:2, :])
+        for u in range(2):
+            nc.sync.dma_start(out=v_late[u][:], in_=v_rows[:, 2 + u, :])
+        nc.sync.dma_start(out=xm_raw[:], in_=xm_rows)
 
         x_bf = sb("x_bf", [P, R * PACK], BF16)
         x_codes = sb("x_codes", [P, R], U32)
         x_scales = sb("x_scales", [P, R], U8)
-        nc.vector.tensor_copy(
+        nc.scalar.copy(
             out=x_bf[:].rearrange("p (t m j) -> p t m j", t=PACK, j=PACK),
             in_=x_raw[:].rearrange("p j (m t) -> p t m j", t=PACK),
         )
@@ -92,13 +96,13 @@ def tile_attend_ghv_lch_kernel(tc, xT, wT, vT, y, wt, xm, offs, out):
         w_codes = sb("w_codes", [P, N], U32)
         w_scales = sb("w_scales", [P, N], U8)
         for t in range(PACK):
-            nc.vector.tensor_copy(w_got[:, t, :], w_pl[t][:].indirect(offsets[:]))
+            nc.vector.tensor_copy(w_got[:, t, :], w_pl[t].indirect(offsets[:]))
         for n in range(PACK):
             interleave(nc.vector.tensor_copy if n < 2 else nc.scalar.copy, w_bf[:, quarter[n], :], w_got[:, :, quarter[n]])
         for n in range(PACK):
             quantize(w_codes, w_scales, w_bf, quarter[n], E4M3)
 
-        z = sb("z", [P, N, PACK], F32)
+        z = sb("z", [P, PACK, PACK, Q], F32)
         q = sb("q", [P, N, PACK], F32)
         q2 = sb("q2", [P, N, PACK], F32)
         h = sb("h", [P, N, PACK], F32)
@@ -106,12 +110,12 @@ def tile_attend_ghv_lch_kernel(tc, xT, wT, vT, y, wt, xm, offs, out):
             cols = slice(n * Q, (n + 1) * Q)
             a = scores(f"bank{n}", w_codes, w_scales, n)
             nc.vector.tensor_tensor(
-                out=z[:, cols, :],
-                in0=a[:].rearrange("p t i -> p i t"),
-                in1=y_sb[:, :, cols].rearrange("p t i -> p i t"),
+                out=z[:, n, :, :],
+                in0=a[:],
+                in1=y_sb[:, :, cols],
                 op=ALU.subtract,
             )
-            nc.scalar.activation(out=q[:, cols, :], in_=z[:, cols, :], func=ACT.Tanh)
+            nc.scalar.activation(out=q[:, cols, :], in_=z[:, n, :, :].rearrange("p t i -> p i t"), func=ACT.Tanh)
             nc.scalar.activation(out=q2[:, cols, :], in_=q[:, cols, :], func=ACT.Square)
         for n in range(PACK):
             cols = slice(n * Q, (n + 1) * Q)
@@ -129,11 +133,11 @@ def tile_attend_ghv_lch_kernel(tc, xT, wT, vT, y, wt, xm, offs, out):
         v_scales = sb("v_scales", [P, N], U8)
         v_got = sb("v_got", [P, PACK, N], F32)
         for t in range(PACK - 1):
-            nc.vector.tensor_copy(v_got[:, t, :], v_pl[t][:].indirect(offsets[:]))
+            nc.vector.tensor_copy(v_got[:, t, :], v_pl[t].indirect(offsets[:]))
 
         def gather_last(half):
             cols = slice(half * N // 2, (half + 1) * N // 2)
-            nc.vector.tensor_copy(v_got[:, PACK - 1, cols], v_pl[PACK - 1][:].indirect(offsets[:, half * 16 : (half + 1) * 16]))
+            nc.vector.tensor_copy(v_got[:, PACK - 1, cols], v_pl[PACK - 1].indirect(offsets[:, half * 16 : (half + 1) * 16]))
 
         def interleave_v(copy, n):
             interleave(copy, v_bf[:, quarter[n], :], v_got[:, :, quarter[n]])
@@ -154,7 +158,7 @@ def tile_attend_ghv_lch_kernel(tc, xT, wT, vT, y, wt, xm, offs, out):
         xm_scales = sb("xm_scales", [P, D], U8)
 
         def cast_xm(m):
-            src = xm_head[:] if m == 0 else xm_rest[:, :, (m - 1) * P : m * P]
+            src = xm_raw[:, :, m * P : (m + 1) * P]
             nc.scalar.copy(
                 out=xm_bf[:, m * P : (m + 1) * P, :].rearrange("p (c i) t -> p c t i", i=4),
                 in_=src.rearrange("p t (c i) -> p c t i", i=4),
@@ -166,42 +170,63 @@ def tile_attend_ghv_lch_kernel(tc, xT, wT, vT, y, wt, xm, offs, out):
                 out=xm_codes[:, cols].bitcast(E4M3), scales=xm_scales[:, cols], in_=xm_bf[:, cols, :].rearrange("p d t -> p (d t)")
             )
 
+        HALF = N // 2
         cast_xm(0)
         g_bf = sb("g_bf", [P, N, PACK], BF16)
-        g_codes = sb("g_codes", [P, N], U32)
-        g_scales = sb("g_scales", [P, N], U8)
-        for n in range(PACK):
-            cols = slice(n * Q, (n + 1) * Q)
-            av = scores(f"bank{PACK + n}", v_codes, v_scales, n)
-            nc.vector.tensor_tensor(out=g_bf[:, cols, :], in0=av[:].rearrange("p t i -> p i t"), in1=h[:, cols, :], op=ALU.mult)
-        quantize_xm(0)
-        nc.vector.quantize_mx(out=g_codes[:].bitcast(E5M2), scales=g_scales[:], in_=g_bf[:].rearrange("p n t -> p (n t)"))
-        for m in range(1, PACK):
-            cast_xm(m)
+        g_codes = sb("g_codes", [P, HALF + N], U32)
+        g_scales = sb("g_scales", [P, HALF + N], U8)
+        nc.gpsimd.memset(g_codes[:, 0:HALF], 0)
+        nc.gpsimd.memset(g_scales[:, 0:HALF], 0)
 
-        for m in range(D // P):
+        def form_g(n):
+            av = scores(f"bank{PACK + n}", v_codes, v_scales, n)
+            nc.vector.tensor_tensor(out=g_bf[:, quarter[n], :], in0=av[:].rearrange("p t i -> p i t"), in1=h[:, quarter[n], :], op=ALU.mult)
+
+        def quantize_g(lo, hi):
+            nc.vector.quantize_mx(
+                out=g_codes[:, HALF + lo : HALF + hi].bitcast(E5M2),
+                scales=g_scales[:, HALF + lo : HALF + hi],
+                in_=g_bf[:, lo:hi, :].rearrange("p n t -> p (n t)"),
+            )
+
+        def product(name, m, lo):
+            dw = psum.tile([P, N], F32, name=name)
             cols = slice(m * P, (m + 1) * P)
-            if m > 0:
-                quantize_xm(m)
-            dw = psum.tile([P, N], F32, name=f"bank{m}")
             nc.tensor.matmul_mx(
                 out=dw[:],
                 lhsT=xm_codes[:, cols].bitcast(E4M3),
                 lhsT_scale=xm_scales[:, cols],
-                rhs=g_codes[:].bitcast(E5M2),
-                rhs_scale=g_scales[:],
+                rhs=g_codes[:, lo : lo + N].bitcast(E5M2),
+                rhs_scale=g_scales[:, lo : lo + N],
                 start=True,
                 stop=True,
             )
-            dense = sb(f"dense{m}", [P, N], F32)
-            wide = sb(f"wide{m}", [P, T], F32)
-            nc.vector.memset(wide[:].bitcast(mybir.dt.int32), 0)
-            if m == 0:
-                for half in range(2):
-                    hc = slice(half * N // 2, (half + 1) * N // 2)
-                    nc.scalar.copy(out=dense[:, hc], in_=dw[:, hc])
-                    nc.vector.tensor_copy(wide[:].indirect(offsets[:, half * 16 : (half + 1) * 16]), dense[:, hc])
-            else:
-                nc.scalar.copy(out=dense[:], in_=dw[:])
-                nc.vector.tensor_copy(wide[:].indirect(offsets[:]), dense[:])
-            nc.sync.dma_start(out=out[cols, :], in_=wide[:])
+            return dw
+
+        dense = [sb(f"dense{m}", [P, N], F32) for m in range(PACK)]
+        wide = [sb(f"wide{m}", [P, T], F32) for m in range(PACK)]
+        for m in range(PACK):
+            nc.gpsimd.memset(wide[m][:], 0.0)
+
+        form_g(0)
+        form_g(1)
+        quantize_xm(0)
+        quantize_g(0, HALF)
+        early = product("bank0", 0, 0)
+        nc.scalar.copy(out=dense[0][:, 0:HALF], in_=early[:, HALF:N])
+        form_g(2)
+        form_g(3)
+        quantize_g(HALF, HALF + Q)
+        quantize_g(HALF + Q, N)
+        late = product("bank1", 0, HALF)
+        nc.scalar.copy(out=dense[0][:, HALF:N], in_=late[:, HALF:N])
+        nc.vector.tensor_copy(wide[0][:].indirect(offsets[:, 0:16]), dense[0][:, 0:HALF])
+        nc.vector.tensor_copy(wide[0][:].indirect(offsets[:, 16:32]), dense[0][:, HALF:N])
+        nc.sync.dma_start(out=out[0:P, :], in_=wide[0][:])
+        for m in range(1, PACK):
+            cast_xm(m)
+            quantize_xm(m)
+            dw = product(f"bank{(m + 1) % PACK}", m, HALF)
+            nc.scalar.copy(out=dense[m][:], in_=dw[:])
+            nc.vector.tensor_copy(wide[m][:].indirect(offsets[:]), dense[m][:])
+            nc.sync.dma_start(out=out[m * P : (m + 1) * P, :], in_=wide[m][:])

@@ -17,7 +17,12 @@ ACT = mybir.ActivationFunctionType
 
 P = 128
 PACK = 4
-Q = 128
+QUARTERS = 4
+Q = N // QUARTERS
+HALF = N // 2
+PER_COLUMN = 16
+BLOCKS = D // P
+ON_VECTOR = (0, 2)
 
 
 def tile_attend_ghv_lch_kernel(tc, xT, wT, vT, y, wt, xm, offs, out):
@@ -29,21 +34,25 @@ def tile_attend_ghv_lch_kernel(tc, xT, wT, vT, y, wt, xm, offs, out):
         def sb(name, shape, dtype):
             return keep.tile(shape, dtype, name=name, align_bytes=64)
 
-        offsets = keep.tile([P, N // 16], U16, name="offsets")
+        quarter = [slice(n * Q, (n + 1) * Q) for n in range(QUARTERS)]
+        half = [slice(0, HALF), slice(HALF, N)]
+        block = [slice(m * P, (m + 1) * P) for m in range(BLOCKS)]
+
+        offsets = keep.tile([P, N // PER_COLUMN], U16, name="offsets")
+        half_offsets = [offsets[:, 0 : HALF // PER_COLUMN], offsets[:, HALF // PER_COLUMN : N // PER_COLUMN]]
         x_raw = sb("x_raw", [P, PACK, R], F32)
         w_pair = sb("w_pair", [P, 2, T], F32)
         w_late = [sb(f"w_late{u}", [P, T], F32) for u in range(2)]
         v_pair = sb("v_pair", [P, 2, T], F32)
         v_late = [sb(f"v_late{u}", [P, T], F32) for u in range(2)]
-        w_pl = [w_pair[:, 0, :], w_pair[:, 1, :], w_late[0][:], w_late[1][:]]
-        v_pl = [v_pair[:, 0, :], v_pair[:, 1, :], v_late[0][:], v_late[1][:]]
+        w_plane = [w_pair[:, 0, :], w_pair[:, 1, :], w_late[0][:], w_late[1][:]]
+        v_plane = [v_pair[:, 0, :], v_pair[:, 1, :], v_late[0][:], v_late[1][:]]
         y_sb = sb("y_sb", [P, PACK, N], F32)
         wt_sb = sb("wt_sb", [P, PACK], F32)
         xm_raw = sb("xm_raw", [P, PACK, D], F32)
 
         w_rows = wT.rearrange("(p t) c -> p t c", t=PACK)
         v_rows = vT.rearrange("(p t) c -> p t c", t=PACK)
-        xm_rows = xm.rearrange("b (p t) d -> p (b t) d", t=PACK)
         nc.sync.dma_start(out=x_raw[:], in_=xT.rearrange("b (p t) r -> p (b t) r", t=PACK))
         nc.sync.dma_start(offsets[:], offs)
         nc.sync.dma_start(out=w_pair[:], in_=w_rows[:, 0:2, :])
@@ -54,7 +63,7 @@ def tile_attend_ghv_lch_kernel(tc, xT, wT, vT, y, wt, xm, offs, out):
         nc.sync.dma_start(out=v_pair[:], in_=v_rows[:, 0:2, :])
         for u in range(2):
             nc.sync.dma_start(out=v_late[u][:], in_=v_rows[:, 2 + u, :])
-        nc.sync.dma_start(out=xm_raw[:], in_=xm_rows)
+        nc.sync.dma_start(out=xm_raw[:], in_=xm.rearrange("b (p t) d -> p (b t) d", t=PACK))
 
         x_bf = sb("x_bf", [P, R * PACK], BF16)
         x_codes = sb("x_codes", [P, R], U32)
@@ -68,60 +77,67 @@ def tile_attend_ghv_lch_kernel(tc, xT, wT, vT, y, wt, xm, offs, out):
         neg_wt = sb("neg_wt", [P, PACK], F32)
         nc.vector.tensor_scalar(out=neg_wt[:], in0=wt_sb[:], scalar1=-1.0, scalar2=None, op0=ALU.mult)
 
-        def scores(name, codes, scales, n):
-            bank = psum.tile([P, PACK, Q], F32, name=name)
-            cols = slice(n * Q, (n + 1) * Q)
+        def scores(bank_name, codes, scales, n):
+            bank = psum.tile([P, PACK, Q], F32, name=bank_name)
             for t in range(PACK):
-                rows = slice(t * P, (t + 1) * P)
+                x_cols = slice(t * P, (t + 1) * P)
                 nc.tensor.matmul_mx(
                     out=bank[:, t, :],
-                    lhsT=x_codes[:, rows].bitcast(E4M3),
-                    lhsT_scale=x_scales[:, rows],
-                    rhs=codes[:, cols].bitcast(E4M3),
-                    rhs_scale=scales[:, cols],
+                    lhsT=x_codes[:, x_cols].bitcast(E4M3),
+                    lhsT_scale=x_scales[:, x_cols],
+                    rhs=codes[:, quarter[n]].bitcast(E4M3),
+                    rhs_scale=scales[:, quarter[n]],
                     start=True,
                     stop=True,
                 )
             return bank
 
-        def interleave(copy, dst, src):
-            copy(out=dst.rearrange("p (c i) t -> p c t i", i=4), in_=src.rearrange("p t (c i) -> p c t i", i=4))
+        def interleave(on_vector, dst, src):
+            if on_vector:
+                nc.vector.tensor_copy(out=dst, in_=src.rearrange("p t c -> p c t"))
+            else:
+                nc.scalar.copy(
+                    out=dst.rearrange("p (c i) t -> p c t i", i=4),
+                    in_=src.rearrange("p t (c i) -> p c t i", i=4),
+                )
 
-        def quantize(codes, scales, src, cols, fmt):
-            nc.vector.quantize_mx(out=codes[:, cols].bitcast(fmt), scales=scales[:, cols], in_=src[:, cols, :].rearrange("p n t -> p (n t)"))
+        def quantize(codes, scales, src, cols):
+            nc.vector.quantize_mx(
+                out=codes[:, cols].bitcast(E4M3),
+                scales=scales[:, cols],
+                in_=src[:, cols, :].rearrange("p c t -> p (c t)"),
+            )
 
-        quarter = [slice(n * Q, (n + 1) * Q) for n in range(PACK)]
         w_got = sb("w_got", [P, PACK, N], F32)
         w_bf = sb("w_bf", [P, N, PACK], BF16)
         w_codes = sb("w_codes", [P, N], U32)
         w_scales = sb("w_scales", [P, N], U8)
         for t in range(PACK):
-            nc.vector.tensor_copy(w_got[:, t, :], w_pl[t].indirect(offsets[:]))
-        for n in range(PACK):
-            interleave(nc.vector.tensor_copy if n < 2 else nc.scalar.copy, w_bf[:, quarter[n], :], w_got[:, :, quarter[n]])
-        for n in range(PACK):
-            quantize(w_codes, w_scales, w_bf, quarter[n], E4M3)
+            nc.vector.tensor_copy(w_got[:, t, :], w_plane[t].indirect(offsets[:]))
+        for n in range(QUARTERS):
+            interleave(n in ON_VECTOR, w_bf[:, quarter[n], :], w_got[:, :, quarter[n]])
+        for n in range(QUARTERS):
+            quantize(w_codes, w_scales, w_bf, quarter[n])
 
-        z = sb("z", [P, PACK, PACK, Q], F32)
+        z = sb("z", [P, N, PACK], F32)
         q = sb("q", [P, N, PACK], F32)
         q2 = sb("q2", [P, N, PACK], F32)
         h = sb("h", [P, N, PACK], F32)
-        for n in range(PACK):
-            cols = slice(n * Q, (n + 1) * Q)
+        for n in range(QUARTERS):
             a = scores(f"bank{n}", w_codes, w_scales, n)
             nc.vector.tensor_tensor(
-                out=z[:, n, :, :],
-                in0=a[:],
-                in1=y_sb[:, :, cols],
+                out=z[:, quarter[n], :],
+                in0=a[:].rearrange("p t i -> p i t"),
+                in1=y_sb[:, :, quarter[n]].rearrange("p t i -> p i t"),
                 op=ALU.subtract,
             )
-            nc.scalar.activation(out=q[:, cols, :], in_=z[:, n, :, :].rearrange("p t i -> p i t"), func=ACT.Tanh)
-            nc.scalar.activation(out=q2[:, cols, :], in_=q[:, cols, :], func=ACT.Square)
-        for n in range(PACK):
-            cols = slice(n * Q, (n + 1) * Q)
+            nc.scalar.activation(out=q[:, quarter[n], :], in_=z[:, quarter[n], :], func=ACT.Tanh)
+            nc.scalar.activation(out=q2[:, quarter[n], :], in_=q[:, quarter[n], :], func=ACT.Square)
+
+        def form_h(n):
             nc.vector.scalar_tensor_tensor(
-                out=h[:, cols, :],
-                in0=q2[:, cols, :],
+                out=h[:, quarter[n], :],
+                in0=q2[:, quarter[n], :],
                 scalar=1.0,
                 in1=neg_wt[:].unsqueeze(1).to_broadcast([P, Q, PACK]),
                 op0=ALU.subtract,
@@ -131,47 +147,30 @@ def tile_attend_ghv_lch_kernel(tc, xT, wT, vT, y, wt, xm, offs, out):
         v_bf = sb("v_bf", [P, N, PACK], BF16)
         v_codes = sb("v_codes", [P, N], U32)
         v_scales = sb("v_scales", [P, N], U8)
-        v_got = sb("v_got", [P, PACK, N], F32)
-        for t in range(PACK - 1):
-            nc.vector.tensor_copy(v_got[:, t, :], v_pl[t].indirect(offsets[:]))
+        v_got = sb("staging", [P, PACK, N], F32)
 
-        def gather_last(half):
-            cols = slice(half * N // 2, (half + 1) * N // 2)
-            nc.vector.tensor_copy(v_got[:, PACK - 1, cols], v_pl[PACK - 1].indirect(offsets[:, half * 16 : (half + 1) * 16]))
+        def gather_v(t):
+            nc.vector.tensor_copy(v_got[:, t, :], v_plane[t].indirect(offsets[:]))
 
-        def interleave_v(copy, n):
-            interleave(copy, v_bf[:, quarter[n], :], v_got[:, :, quarter[n]])
+        form_h(0)
+        form_h(1)
+        gather_v(0)
+        gather_v(1)
+        form_h(2)
+        gather_v(2)
+        form_h(3)
+        for u in range(2):
+            nc.vector.tensor_copy(v_got[:, PACK - 1, half[u]], v_plane[PACK - 1].indirect(half_offsets[u]))
+        for n in range(QUARTERS):
+            interleave(n in ON_VECTOR, v_bf[:, quarter[n], :], v_got[:, :, quarter[n]])
+        for n in range(QUARTERS):
+            quantize(v_codes, v_scales, v_bf, quarter[n])
 
-        gather_last(0)
-        interleave_v(nc.vector.tensor_copy, 0)
-        interleave_v(nc.scalar.copy, 1)
-        gather_last(1)
-        interleave_v(nc.scalar.copy, 2)
-        quantize(v_codes, v_scales, v_bf, quarter[0], E4M3)
-        quantize(v_codes, v_scales, v_bf, quarter[1], E4M3)
-        interleave_v(nc.vector.tensor_copy, 3)
-        quantize(v_codes, v_scales, v_bf, quarter[2], E4M3)
-        quantize(v_codes, v_scales, v_bf, quarter[3], E4M3)
-
-        xm_bf = sb("xm_bf", [P, D, PACK], BF16)
+        xm_bf = sb("staging", [P, D, PACK], BF16)
         xm_codes = sb("xm_codes", [P, D], U32)
         xm_scales = sb("xm_scales", [P, D], U8)
+        interleave(False, xm_bf[:, block[0], :], xm_raw[:, :, block[0]])
 
-        def cast_xm(m):
-            src = xm_raw[:, :, m * P : (m + 1) * P]
-            nc.scalar.copy(
-                out=xm_bf[:, m * P : (m + 1) * P, :].rearrange("p (c i) t -> p c t i", i=4),
-                in_=src.rearrange("p t (c i) -> p c t i", i=4),
-            )
-
-        def quantize_xm(m):
-            cols = slice(m * P, (m + 1) * P)
-            nc.vector.quantize_mx(
-                out=xm_codes[:, cols].bitcast(E4M3), scales=xm_scales[:, cols], in_=xm_bf[:, cols, :].rearrange("p d t -> p (d t)")
-            )
-
-        HALF = N // 2
-        cast_xm(0)
         g_bf = sb("g_bf", [P, N, PACK], BF16)
         g_codes = sb("g_codes", [P, HALF + N], U32)
         g_scales = sb("g_scales", [P, HALF + N], U8)
@@ -179,54 +178,59 @@ def tile_attend_ghv_lch_kernel(tc, xT, wT, vT, y, wt, xm, offs, out):
         nc.gpsimd.memset(g_scales[:, 0:HALF], 0)
 
         def form_g(n):
-            av = scores(f"bank{PACK + n}", v_codes, v_scales, n)
-            nc.vector.tensor_tensor(out=g_bf[:, quarter[n], :], in0=av[:].rearrange("p t i -> p i t"), in1=h[:, quarter[n], :], op=ALU.mult)
-
-        def quantize_g(lo, hi):
-            nc.vector.quantize_mx(
-                out=g_codes[:, HALF + lo : HALF + hi].bitcast(E5M2),
-                scales=g_scales[:, HALF + lo : HALF + hi],
-                in_=g_bf[:, lo:hi, :].rearrange("p n t -> p (n t)"),
+            av = scores(f"bank{QUARTERS + n}", v_codes, v_scales, n)
+            nc.vector.tensor_tensor(
+                out=g_bf[:, quarter[n], :],
+                in0=av[:].rearrange("p t i -> p i t"),
+                in1=h[:, quarter[n], :],
+                op=ALU.mult,
             )
 
-        def product(name, m, lo):
-            dw = psum.tile([P, N], F32, name=name)
-            cols = slice(m * P, (m + 1) * P)
+        def quantize_g(first, last):
+            nc.vector.quantize_mx(
+                out=g_codes[:, HALF + first : HALF + last].bitcast(E5M2),
+                scales=g_scales[:, HALF + first : HALF + last],
+                in_=g_bf[:, first:last, :].rearrange("p i t -> p (i t)"),
+            )
+
+        def product(bank_name, m, first_col):
+            dw = psum.tile([P, N], F32, name=bank_name)
             nc.tensor.matmul_mx(
                 out=dw[:],
-                lhsT=xm_codes[:, cols].bitcast(E4M3),
-                lhsT_scale=xm_scales[:, cols],
-                rhs=g_codes[:, lo : lo + N].bitcast(E5M2),
-                rhs_scale=g_scales[:, lo : lo + N],
+                lhsT=xm_codes[:, block[m]].bitcast(E4M3),
+                lhsT_scale=xm_scales[:, block[m]],
+                rhs=g_codes[:, first_col : first_col + N].bitcast(E5M2),
+                rhs_scale=g_scales[:, first_col : first_col + N],
                 start=True,
                 stop=True,
             )
             return dw
 
-        dense = [sb(f"dense{m}", [P, N], F32) for m in range(PACK)]
-        wide = [sb(f"wide{m}", [P, T], F32) for m in range(PACK)]
-        for m in range(PACK):
+        dense = [sb(f"dense{m}", [P, N], F32) for m in range(BLOCKS)]
+        wide = [sb(f"wide{m}", [P, T], F32) for m in range(BLOCKS)]
+        for m in range(BLOCKS):
             nc.gpsimd.memset(wide[m][:], 0.0)
 
         form_g(0)
         form_g(1)
-        quantize_xm(0)
+        quantize(xm_codes, xm_scales, xm_bf, block[0])
         quantize_g(0, HALF)
-        early = product("bank0", 0, 0)
-        nc.scalar.copy(out=dense[0][:, 0:HALF], in_=early[:, HALF:N])
+        first = product("bank0", 0, 0)
+        nc.scalar.copy(out=dense[0][:, half[0]], in_=first[:, half[1]])
         form_g(2)
         form_g(3)
         quantize_g(HALF, HALF + Q)
         quantize_g(HALF + Q, N)
-        late = product("bank1", 0, HALF)
-        nc.scalar.copy(out=dense[0][:, HALF:N], in_=late[:, HALF:N])
-        nc.vector.tensor_copy(wide[0][:].indirect(offsets[:, 0:16]), dense[0][:, 0:HALF])
-        nc.vector.tensor_copy(wide[0][:].indirect(offsets[:, 16:32]), dense[0][:, HALF:N])
-        nc.sync.dma_start(out=out[0:P, :], in_=wide[0][:])
-        for m in range(1, PACK):
-            cast_xm(m)
-            quantize_xm(m)
-            dw = product(f"bank{(m + 1) % PACK}", m, HALF)
+        second = product("bank1", 0, HALF)
+        nc.scalar.copy(out=dense[0][:, half[1]], in_=second[:, half[1]])
+        nc.vector.tensor_copy(wide[0][:].indirect(half_offsets[0]), dense[0][:, half[0]])
+        for m in range(1, BLOCKS):
+            interleave(False, xm_bf[:, block[m], :], xm_raw[:, :, block[m]])
+            quantize(xm_codes, xm_scales, xm_bf, block[m])
+        nc.vector.tensor_copy(wide[0][:].indirect(half_offsets[1]), dense[0][:, half[1]])
+        nc.sync.dma_start(out=out[block[0], :], in_=wide[0][:])
+        for m in range(1, BLOCKS):
+            dw = product(f"bank{(m + 1) % QUARTERS}", m, HALF)
             nc.scalar.copy(out=dense[m][:], in_=dw[:])
             nc.vector.tensor_copy(wide[m][:].indirect(offsets[:]), dense[m][:])
-            nc.sync.dma_start(out=out[m * P : (m + 1) * P, :], in_=wide[m][:])
+            nc.sync.dma_start(out=out[block[m], :], in_=wide[m][:])

@@ -112,8 +112,10 @@ def tile_attend_ghv_lch_kernel(tc, xT, wT, vT, y, wt, xm, offs, out):
         w_bf = sb("w_bf", [P, N, PACK], BF16)
         w_codes = sb("w_codes", [P, N], U32)
         w_scales = sb("w_scales", [P, N], U8)
-        for t in range(PACK):
+        for t in range(PACK - 1):
             nc.vector.tensor_copy(w_got[:, t, :], w_plane[t].indirect(offsets[:]))
+        for u in range(2):
+            nc.vector.tensor_copy(w_got[:, PACK - 1, half[u]], w_plane[PACK - 1].indirect(half_offsets[u]))
         for n in range(QUARTERS):
             interleave(n in ON_VECTOR, w_bf[:, quarter[n], :], w_got[:, :, quarter[n]])
         for n in range(QUARTERS):
@@ -122,7 +124,11 @@ def tile_attend_ghv_lch_kernel(tc, xT, wT, vT, y, wt, xm, offs, out):
         z = sb("z", [P, N, PACK], F32)
         q = sb("q", [P, N, PACK], F32)
         q2 = sb("q2", [P, N, PACK], F32)
-        h = sb("h", [P, N, PACK], F32)
+        h = [sb(f"h{n}", [P, Q, PACK], F32) for n in range(QUARTERS - 1)]
+
+        def square(n):
+            nc.scalar.activation(out=q2[:, quarter[n], :], in_=q[:, quarter[n], :], func=ACT.Square)
+
         for n in range(QUARTERS):
             a = scores(f"bank{n}", w_codes, w_scales, n)
             nc.vector.tensor_tensor(
@@ -132,11 +138,13 @@ def tile_attend_ghv_lch_kernel(tc, xT, wT, vT, y, wt, xm, offs, out):
                 op=ALU.subtract,
             )
             nc.scalar.activation(out=q[:, quarter[n], :], in_=z[:, quarter[n], :], func=ACT.Tanh)
-            nc.scalar.activation(out=q2[:, quarter[n], :], in_=q[:, quarter[n], :], func=ACT.Square)
+            if n > 0:
+                square(n - 1)
+        square(QUARTERS - 1)
 
         def form_h(n):
             nc.vector.scalar_tensor_tensor(
-                out=h[:, quarter[n], :],
+                out=h[n][:],
                 in0=q2[:, quarter[n], :],
                 scalar=1.0,
                 in1=neg_wt[:].unsqueeze(1).to_broadcast([P, Q, PACK]),
@@ -144,7 +152,7 @@ def tile_attend_ghv_lch_kernel(tc, xT, wT, vT, y, wt, xm, offs, out):
                 op1=ALU.mult,
             )
 
-        v_bf = sb("v_bf", [P, N, PACK], BF16)
+        v_bf = [sb(f"v_bf{n}", [P, Q, PACK], BF16) for n in range(QUARTERS)]
         v_codes = sb("v_codes", [P, N], U32)
         v_scales = sb("v_scales", [P, N], U8)
         v_got = sb("staging", [P, PACK, N], F32)
@@ -158,13 +166,18 @@ def tile_attend_ghv_lch_kernel(tc, xT, wT, vT, y, wt, xm, offs, out):
         gather_v(1)
         form_h(2)
         gather_v(2)
-        form_h(3)
         for u in range(2):
             nc.vector.tensor_copy(v_got[:, PACK - 1, half[u]], v_plane[PACK - 1].indirect(half_offsets[u]))
         for n in range(QUARTERS):
-            interleave(n in ON_VECTOR, v_bf[:, quarter[n], :], v_got[:, :, quarter[n]])
+            interleave(n in ON_VECTOR, v_bf[n][:], v_got[:, :, quarter[n]])
         for n in range(QUARTERS):
-            quantize(v_codes, v_scales, v_bf, quarter[n])
+            nc.vector.quantize_mx(
+                out=v_codes[:, quarter[n]].bitcast(E4M3),
+                scales=v_scales[:, quarter[n]],
+                in_=v_bf[n][:].rearrange("p c t -> p (c t)"),
+            )
+        h.append(sb("v_bf0", [P, Q, PACK], F32))
+        form_h(QUARTERS - 1)
 
         xm_bf = sb("staging", [P, D, PACK], BF16)
         xm_codes = sb("xm_codes", [P, D], U32)
@@ -182,7 +195,7 @@ def tile_attend_ghv_lch_kernel(tc, xT, wT, vT, y, wt, xm, offs, out):
             nc.vector.tensor_tensor(
                 out=g_bf[:, quarter[n], :],
                 in0=av[:].rearrange("p t i -> p i t"),
-                in1=h[:, quarter[n], :],
+                in1=h[n][:],
                 op=ALU.mult,
             )
 

@@ -22,7 +22,6 @@ Q = N // QUARTERS
 HALF = N // 2
 PER_COLUMN = 16
 BLOCKS = D // P
-ON_VECTOR = (0, 2)
 
 
 def tile_attend_ghv_lch_kernel(tc, xT, wT, vT, y, wt, xm, offs, out):
@@ -108,6 +107,15 @@ def tile_attend_ghv_lch_kernel(tc, xT, wT, vT, y, wt, xm, offs, out):
                 in_=src[:, cols, :].rearrange("p c t -> p (c t)"),
             )
 
+        def prepare(codes, scales, bf, got):
+            interleave(True, bf[:, quarter[0], :], got[:, :, quarter[0]])
+            interleave(False, bf[:, quarter[1], :], got[:, :, quarter[1]])
+            interleave(True, bf[:, quarter[2], :], got[:, :, quarter[2]])
+            quantize(codes, scales, bf, quarter[0])
+            interleave(True, bf[:, quarter[3], :], got[:, :, quarter[3]])
+            for n in range(1, QUARTERS):
+                quantize(codes, scales, bf, quarter[n])
+
         w_got = sb("w_got", [P, PACK, N], F32)
         w_bf = sb("w_bf", [P, N, PACK], BF16)
         w_codes = sb("w_codes", [P, N], U32)
@@ -116,15 +124,12 @@ def tile_attend_ghv_lch_kernel(tc, xT, wT, vT, y, wt, xm, offs, out):
             nc.vector.tensor_copy(w_got[:, t, :], w_plane[t].indirect(offsets[:]))
         for u in range(2):
             nc.vector.tensor_copy(w_got[:, PACK - 1, half[u]], w_plane[PACK - 1].indirect(half_offsets[u]))
-        for n in range(QUARTERS):
-            interleave(n in ON_VECTOR, w_bf[:, quarter[n], :], w_got[:, :, quarter[n]])
-        for n in range(QUARTERS):
-            quantize(w_codes, w_scales, w_bf, quarter[n])
+        prepare(w_codes, w_scales, w_bf, w_got)
 
         z = sb("z", [P, N, PACK], F32)
         q = sb("q", [P, N, PACK], F32)
         q2 = sb("q2", [P, N, PACK], F32)
-        h = [sb(f"h{n}", [P, Q, PACK], F32) for n in range(QUARTERS - 1)]
+        h = sb("h", [P, N, PACK], F32)
 
         def square(n):
             nc.scalar.activation(out=q2[:, quarter[n], :], in_=q[:, quarter[n], :], func=ACT.Square)
@@ -144,7 +149,7 @@ def tile_attend_ghv_lch_kernel(tc, xT, wT, vT, y, wt, xm, offs, out):
 
         def form_h(n):
             nc.vector.scalar_tensor_tensor(
-                out=h[n][:],
+                out=h[:, quarter[n], :],
                 in0=q2[:, quarter[n], :],
                 scalar=1.0,
                 in1=neg_wt[:].unsqueeze(1).to_broadcast([P, Q, PACK]),
@@ -152,7 +157,7 @@ def tile_attend_ghv_lch_kernel(tc, xT, wT, vT, y, wt, xm, offs, out):
                 op1=ALU.mult,
             )
 
-        v_bf = [sb(f"v_bf{n}", [P, Q, PACK], BF16) for n in range(QUARTERS)]
+        v_bf = sb("v_bf", [P, N, PACK], BF16)
         v_codes = sb("v_codes", [P, N], U32)
         v_scales = sb("v_scales", [P, N], U8)
         v_got = sb("staging", [P, PACK, N], F32)
@@ -165,45 +170,51 @@ def tile_attend_ghv_lch_kernel(tc, xT, wT, vT, y, wt, xm, offs, out):
         gather_v(0)
         gather_v(1)
         form_h(2)
+        form_h(3)
         gather_v(2)
         for u in range(2):
             nc.vector.tensor_copy(v_got[:, PACK - 1, half[u]], v_plane[PACK - 1].indirect(half_offsets[u]))
-        for n in range(QUARTERS):
-            interleave(n in ON_VECTOR, v_bf[n][:], v_got[:, :, quarter[n]])
-        for n in range(QUARTERS):
-            nc.vector.quantize_mx(
-                out=v_codes[:, quarter[n]].bitcast(E4M3),
-                scales=v_scales[:, quarter[n]],
-                in_=v_bf[n][:].rearrange("p c t -> p (c t)"),
-            )
-        h.append(sb("v_bf0", [P, Q, PACK], F32))
-        form_h(QUARTERS - 1)
+        prepare(v_codes, v_scales, v_bf, v_got)
 
-        xm_bf = sb("staging", [P, D, PACK], BF16)
         xm_codes = sb("xm_codes", [P, D], U32)
         xm_scales = sb("xm_scales", [P, D], U8)
-        interleave(False, xm_bf[:, block[0], :], xm_raw[:, :, block[0]])
 
-        g_bf = sb("g_bf", [P, N, PACK], BF16)
+        def round_xm(on_vector, tile_name, m):
+            bf = sb(tile_name, [P, P, PACK], BF16)
+            interleave(on_vector, bf[:], xm_raw[:, :, block[m]])
+            return bf
+
+        def quantize_xm(bf, m):
+            nc.vector.quantize_mx(
+                out=xm_codes[:, block[m]].bitcast(E4M3),
+                scales=xm_scales[:, block[m]],
+                in_=bf[:].rearrange("p c t -> p (c t)"),
+            )
+
+        xm_bf0 = round_xm(False, "staging", 0)
+        xm_bf1 = round_xm(False, "xm_bf1", 1)
+
+        g_bf = sb("g_bf", [P, N - Q, PACK], BF16)
+        g_last = sb("g_last", [P, Q, PACK], BF16)
         g_codes = sb("g_codes", [P, HALF + N], U32)
         g_scales = sb("g_scales", [P, HALF + N], U8)
         nc.gpsimd.memset(g_codes[:, 0:HALF], 0)
         nc.gpsimd.memset(g_scales[:, 0:HALF], 0)
 
-        def form_g(n):
+        def form_g(n, dst):
             av = scores(f"bank{QUARTERS + n}", v_codes, v_scales, n)
             nc.vector.tensor_tensor(
-                out=g_bf[:, quarter[n], :],
+                out=dst,
                 in0=av[:].rearrange("p t i -> p i t"),
-                in1=h[n][:],
+                in1=h[:, quarter[n], :],
                 op=ALU.mult,
             )
 
-        def quantize_g(first, last):
+        def quantize_g(first, last, src):
             nc.vector.quantize_mx(
                 out=g_codes[:, HALF + first : HALF + last].bitcast(E5M2),
                 scales=g_scales[:, HALF + first : HALF + last],
-                in_=g_bf[:, first:last, :].rearrange("p i t -> p (i t)"),
+                in_=src.rearrange("p i t -> p (i t)"),
             )
 
         def product(bank_name, m, first_col):
@@ -224,26 +235,32 @@ def tile_attend_ghv_lch_kernel(tc, xT, wT, vT, y, wt, xm, offs, out):
         for m in range(BLOCKS):
             nc.gpsimd.memset(wide[m][:], 0.0)
 
-        form_g(0)
-        form_g(1)
-        quantize(xm_codes, xm_scales, xm_bf, block[0])
-        quantize_g(0, HALF)
+        for n in range(QUARTERS - 1):
+            form_g(n, g_bf[:, quarter[n], :])
+        quantize_g(0, HALF, g_bf[:, half[0], :])
+        quantize_xm(xm_bf0, 0)
         first = product("bank0", 0, 0)
         nc.scalar.copy(out=dense[0][:, half[0]], in_=first[:, half[1]])
-        form_g(2)
-        form_g(3)
-        quantize_g(HALF, HALF + Q)
-        quantize_g(HALF + Q, N)
+        form_g(QUARTERS - 1, g_last[:])
+        quantize_g(HALF, HALF + Q, g_bf[:, quarter[2], :])
+        quantize_g(HALF + Q, N, g_last[:])
         second = product("bank1", 0, HALF)
         nc.scalar.copy(out=dense[0][:, half[1]], in_=second[:, half[1]])
         nc.vector.tensor_copy(wide[0][:].indirect(half_offsets[0]), dense[0][:, half[0]])
-        for m in range(1, BLOCKS):
-            interleave(False, xm_bf[:, block[m], :], xm_raw[:, :, block[m]])
-            quantize(xm_codes, xm_scales, xm_bf, block[m])
+        quantize_xm(xm_bf1, 1)
+        xm_bf2 = round_xm(True, "g_last", 2)
         nc.vector.tensor_copy(wide[0][:].indirect(half_offsets[1]), dense[0][:, half[1]])
         nc.sync.dma_start(out=out[block[0], :], in_=wide[0][:])
-        for m in range(1, BLOCKS):
+        quantize_xm(xm_bf2, 2)
+
+        def finish(m):
             dw = product(f"bank{(m + 1) % QUARTERS}", m, HALF)
             nc.scalar.copy(out=dense[m][:], in_=dw[:])
             nc.vector.tensor_copy(wide[m][:].indirect(offsets[:]), dense[m][:])
             nc.sync.dma_start(out=out[block[m], :], in_=wide[m][:])
+
+        finish(1)
+        xm_bf3 = round_xm(True, "dense0", 3)
+        finish(2)
+        quantize_xm(xm_bf3, 3)
+        finish(3)

@@ -64,6 +64,14 @@ def tile_attend_ghv_lch_kernel(tc, xT, wT, vT, y, wt, xm, offs, out):
             nc.sync.dma_start(out=v_late[u][:], in_=v_rows[:, 2 + u, :])
         nc.sync.dma_start(out=xm_raw[:], in_=xm.rearrange("b (p t) d -> p (b t) d", t=PACK))
 
+        wide = [sb(f"wide{m}", [P, T], F32) for m in range(BLOCKS)]
+        for m in range(BLOCKS):
+            nc.vector.memset(wide[m][:].bitcast(U32), 0)
+        g_codes = sb("g_codes", [P, HALF + N], U32)
+        g_scales = sb("g_scales", [P, HALF + N], U8)
+        nc.vector.memset(g_codes[:, 0:HALF], 0)
+        nc.vector.memset(g_scales[:, 0:HALF].bitcast(U32), 0)
+
         x_bf = sb("x_bf", [P, R * PACK], BF16)
         x_codes = sb("x_codes", [P, R], U32)
         x_scales = sb("x_scales", [P, R], U8)
@@ -196,10 +204,6 @@ def tile_attend_ghv_lch_kernel(tc, xT, wT, vT, y, wt, xm, offs, out):
 
         g_bf = sb("g_bf", [P, N - Q, PACK], BF16)
         g_last = sb("g_last", [P, Q, PACK], BF16)
-        g_codes = sb("g_codes", [P, HALF + N], U32)
-        g_scales = sb("g_scales", [P, HALF + N], U8)
-        nc.gpsimd.memset(g_codes[:, 0:HALF], 0)
-        nc.gpsimd.memset(g_scales[:, 0:HALF], 0)
 
         def form_g(n, dst):
             av = scores(f"bank{QUARTERS + n}", v_codes, v_scales, n)
@@ -231,9 +235,6 @@ def tile_attend_ghv_lch_kernel(tc, xT, wT, vT, y, wt, xm, offs, out):
             return dw
 
         dense = [sb(f"dense{m}", [P, N], F32) for m in range(BLOCKS)]
-        wide = [sb(f"wide{m}", [P, T], F32) for m in range(BLOCKS)]
-        for m in range(BLOCKS):
-            nc.gpsimd.memset(wide[m][:], 0.0)
 
         for n in range(QUARTERS - 1):
             form_g(n, g_bf[:, quarter[n], :])

@@ -57,8 +57,8 @@ def tile_attend_ghv_lch_kernel(tc, xT, wT, vT, y, wt, xm, offs, out):
         nc.sync.dma_start(out=w_pair[:], in_=w_rows[:, 0:2, :])
         for u in range(2):
             nc.sync.dma_start(out=w_late[u][:], in_=w_rows[:, 2 + u, :])
-        nc.sync.dma_start(out=wt_sb[:], in_=wt.rearrange("b (p t) o -> p (b t o)", t=PACK))
         nc.sync.dma_start(out=y_sb[:], in_=y.rearrange("b (p t) i -> p (b t) i", t=PACK))
+        nc.sync.dma_start(out=wt_sb[:], in_=wt.rearrange("b (p t) o -> p (b t o)", t=PACK))
         nc.sync.dma_start(out=v_pair[:], in_=v_rows[:, 0:2, :])
         for u in range(2):
             nc.sync.dma_start(out=v_late[u][:], in_=v_rows[:, 2 + u, :])
@@ -80,9 +80,6 @@ def tile_attend_ghv_lch_kernel(tc, xT, wT, vT, y, wt, xm, offs, out):
             in_=x_raw[:].rearrange("p j (m t) -> p t m j", t=PACK),
         )
         nc.vector.quantize_mx(out=x_codes[:].bitcast(E4M3), scales=x_scales[:], in_=x_bf[:])
-
-        neg_wt = sb("neg_wt", [P, PACK], F32)
-        nc.vector.tensor_scalar(out=neg_wt[:], in0=wt_sb[:], scalar1=-1.0, scalar2=None, op0=ALU.mult)
 
         def scores(bank_name, codes, scales, n):
             bank = psum.tile([P, PACK, Q], F32, name=bank_name)
@@ -155,6 +152,9 @@ def tile_attend_ghv_lch_kernel(tc, xT, wT, vT, y, wt, xm, offs, out):
                 square(n - 1)
         square(QUARTERS - 1)
 
+        neg_wt = sb("neg_wt", [P, PACK], F32)
+        nc.vector.tensor_scalar(out=neg_wt[:], in0=wt_sb[:], scalar1=-1.0, scalar2=None, op0=ALU.mult)
+
         def form_h(n):
             nc.vector.scalar_tensor_tensor(
                 out=h[:, quarter[n], :],
@@ -173,13 +173,10 @@ def tile_attend_ghv_lch_kernel(tc, xT, wT, vT, y, wt, xm, offs, out):
         def gather_v(t):
             nc.vector.tensor_copy(v_got[:, t, :], v_plane[t].indirect(offsets[:]))
 
-        form_h(0)
-        form_h(1)
-        gather_v(0)
-        gather_v(1)
-        form_h(2)
-        form_h(3)
-        gather_v(2)
+        for t in range(PACK - 1):
+            form_h(t)
+            gather_v(t)
+        form_h(QUARTERS - 1)
         for u in range(2):
             nc.vector.tensor_copy(v_got[:, PACK - 1, half[u]], v_plane[PACK - 1].indirect(half_offsets[u]))
         prepare(v_codes, v_scales, v_bf, v_got)

@@ -67,10 +67,12 @@ def tile_attend_ghv_lch_kernel(tc, xT, wT, vT, y, wt, xm, offs, out):
         wide = [sb(f"wide{m}", [P, T], F32) for m in range(BLOCKS)]
         for m in range(BLOCKS):
             nc.vector.memset(wide[m][:].bitcast(U32), 0)
-        g_codes = sb("g_codes", [P, HALF + N], U32)
-        g_scales = sb("g_scales", [P, HALF + N], U8)
-        nc.vector.memset(g_codes[:, 0:HALF], 0)
-        nc.vector.memset(g_scales[:, 0:HALF].bitcast(U32), 0)
+        g_codes = sb("g_codes", [P, Q + N], U32)
+        g_scales = sb("g_scales", [P, Q + N], U8)
+        nc.vector.memset(g_codes[:, 0:Q], 0)
+        nc.vector.memset(g_scales[:, 0:Q].bitcast(U32), 0)
+        zeros = sb("zeros", [P, Q], F32)
+        nc.vector.memset(zeros[:], 0.0)
 
         x_bf = sb("x_bf", [P, R * PACK], BF16)
         x_codes = sb("x_codes", [P, R], U32)
@@ -213,8 +215,8 @@ def tile_attend_ghv_lch_kernel(tc, xT, wT, vT, y, wt, xm, offs, out):
 
         def quantize_g(first, last, src):
             nc.vector.quantize_mx(
-                out=g_codes[:, HALF + first : HALF + last].bitcast(E5M2),
-                scales=g_scales[:, HALF + first : HALF + last],
+                out=g_codes[:, Q + first : Q + last].bitcast(E5M2),
+                scales=g_scales[:, Q + first : Q + last],
                 in_=src.rearrange("p i t -> p (i t)"),
             )
 
@@ -237,22 +239,28 @@ def tile_attend_ghv_lch_kernel(tc, xT, wT, vT, y, wt, xm, offs, out):
             form_g(n, g_bf[:, quarter[n], :])
         quantize_g(0, HALF, g_bf[:, half[0], :])
         quantize_xm(xm_bf0, 0)
+        quantize_g(HALF, N - Q, g_bf[:, quarter[2], :])
         first = product("bank0", 0, 0)
-        nc.scalar.copy(out=dense[0][:, half[0]], in_=first[:, half[1]])
+        nc.scalar.copy(out=dense[0][:, 0 : N - Q], in_=first[:, Q:N])
         form_g(QUARTERS - 1, g_last[:])
-        quantize_g(HALF, HALF + Q, g_bf[:, quarter[2], :])
-        quantize_g(HALF + Q, N, g_last[:])
-        second = product("bank1", 0, HALF)
-        nc.scalar.copy(out=dense[0][:, half[1]], in_=second[:, half[1]])
-        nc.vector.tensor_copy(wide[0][:].indirect(half_offsets[0]), dense[0][:, half[0]])
         quantize_xm(xm_bf1, 1)
+        quantize_g(N - Q, N, g_last[:])
+        second = product("bank1", 0, Q)
+        nc.scalar.copy(out=dense[0][:, quarter[3]], in_=second[:, quarter[3]])
         xm_bf2 = round_xm(True, "g_last", 2)
-        nc.vector.tensor_copy(wide[0][:].indirect(half_offsets[1]), dense[0][:, half[1]])
+        split = (N - Q) // PER_COLUMN
+        nc.vector.tensor_copy(wide[0][:].indirect(offsets[:, 0:split]), dense[0][:, 0 : N - Q])
+        nc.vector.tensor_tensor(
+            out=wide[0][:].indirect(offsets[:, split : N // PER_COLUMN]),
+            in0=dense[0][:, quarter[3]],
+            in1=zeros[:],
+            op=ALU.add,
+        )
         nc.sync.dma_start(out=out[block[0], :], in_=wide[0][:])
         quantize_xm(xm_bf2, 2)
 
         def finish(m):
-            dw = product(f"bank{(m + 1) % QUARTERS}", m, HALF)
+            dw = product(f"bank{(m + 1) % QUARTERS}", m, Q)
             nc.scalar.copy(out=dense[m][:], in_=dw[:])
             nc.vector.tensor_copy(wide[m][:].indirect(offsets[:]), dense[m][:])
             nc.sync.dma_start(out=out[block[m], :], in_=wide[m][:])

@@ -78,8 +78,8 @@ def tile_attend_ghv_lch_kernel(tc, xT, wT, vT, y, wt, xm, offs, out):
         x_codes = sb("x_codes", [P, R], U32)
         x_scales = sb("x_scales", [P, R], U8)
         nc.scalar.copy(
-            out=x_bf[:].rearrange("p (t m j) -> p t m j", t=PACK, j=PACK),
-            in_=x_raw[:].rearrange("p j (m t) -> p t m j", t=PACK),
+            out=x_bf[:].rearrange("p (t m j) -> p m t j", t=PACK, j=PACK),
+            in_=x_raw[:].rearrange("p j (m t) -> p m t j", t=PACK),
         )
         nc.vector.quantize_mx(out=x_codes[:].bitcast(E4M3), scales=x_scales[:], in_=x_bf[:])
 
@@ -144,9 +144,9 @@ def tile_attend_ghv_lch_kernel(tc, xT, wT, vT, y, wt, xm, offs, out):
         for n in range(QUARTERS):
             a = scores(f"bank{n}", w_codes, w_scales, n)
             nc.vector.tensor_tensor(
-                out=z[:, quarter[n], :],
-                in0=a[:].rearrange("p t i -> p i t"),
-                in1=y_sb[:, :, quarter[n]].rearrange("p t i -> p i t"),
+                out=z[:, quarter[n], :].rearrange("p (c i) t -> p c t i", i=4),
+                in0=a[:].rearrange("p t (c i) -> p c t i", i=4),
+                in1=y_sb[:, :, quarter[n]].rearrange("p t (c i) -> p c t i", i=4),
                 op=ALU.subtract,
             )
             nc.scalar.activation(out=q[:, quarter[n], :], in_=z[:, quarter[n], :], func=ACT.Tanh)

@@ -99,13 +99,11 @@ def tile_attend_ghv_lch_kernel(tc, xT, wT, vT, y, wt, xm, offs, out):
             return bank
 
         def interleave(on_vector, dst, src):
-            if on_vector:
-                nc.vector.tensor_copy(out=dst, in_=src.rearrange("p t c -> p c t"))
-            else:
-                nc.scalar.copy(
-                    out=dst.rearrange("p (c i) t -> p c t i", i=4),
-                    in_=src.rearrange("p t (c i) -> p c t i", i=4),
-                )
+            copy = nc.vector.tensor_copy if on_vector else nc.scalar.copy
+            copy(
+                out=dst.rearrange("p (c i) t -> p c t i", i=4),
+                in_=src.rearrange("p t (c i) -> p c t i", i=4),
+            )
 
         def quantize(codes, scales, src, cols):
             nc.vector.quantize_mx(

@@ -48,7 +48,9 @@ def tile_attend_ghv_lch_kernel(tc, xT, wT, vT, y, wt, xm, offs, out):
         v_plane = [v_pair[:, 0, :], v_pair[:, 1, :], v_late[0][:], v_late[1][:]]
         y_sb = sb("y_sb", [P, PACK, N], F32)
         wt_sb = sb("wt_sb", [P, PACK], F32)
-        xm_raw = sb("xm_raw", [P, PACK, D], F32)
+        xm_first = sb("xm_first", [P, PACK, P], F32)
+        xm_rest = sb("xm_rest", [P, PACK, D - P], F32)
+        xm_block = [xm_first[:]] + [xm_rest[:, :, block[m]] for m in range(BLOCKS - 1)]
 
         w_rows = wT.rearrange("(p t) c -> p t c", t=PACK)
         v_rows = vT.rearrange("(p t) c -> p t c", t=PACK)
@@ -62,7 +64,9 @@ def tile_attend_ghv_lch_kernel(tc, xT, wT, vT, y, wt, xm, offs, out):
         nc.sync.dma_start(out=v_pair[:], in_=v_rows[:, 0:2, :])
         for u in range(2):
             nc.sync.dma_start(out=v_late[u][:], in_=v_rows[:, 2 + u, :])
-        nc.sync.dma_start(out=xm_raw[:], in_=xm.rearrange("b (p t) d -> p (b t) d", t=PACK))
+        xm_rows = xm.rearrange("b (p t) d -> p (b t) d", t=PACK)
+        nc.sync.dma_start(out=xm_first[:], in_=xm_rows[:, :, 0:P])
+        nc.sync.dma_start(out=xm_rest[:], in_=xm_rows[:, :, P:D])
 
         wide = [sb(f"wide{m}", [P, T], F32) for m in range(BLOCKS)]
         for m in range(BLOCKS):
@@ -168,7 +172,7 @@ def tile_attend_ghv_lch_kernel(tc, xT, wT, vT, y, wt, xm, offs, out):
         v_bf = sb("v_bf", [P, N, PACK], BF16)
         v_codes = sb("v_codes", [P, N], U32)
         v_scales = sb("v_scales", [P, N], U8)
-        v_got = sb("staging", [P, PACK, N], F32)
+        v_got = sb("v_got", [P, PACK, N], F32)
 
         def gather_v(t):
             nc.vector.tensor_copy(v_got[:, t, :], v_plane[t].indirect(offsets[:]))
@@ -186,7 +190,7 @@ def tile_attend_ghv_lch_kernel(tc, xT, wT, vT, y, wt, xm, offs, out):
 
         def round_xm(on_vector, tile_name, m):
             bf = sb(tile_name, [P, P, PACK], BF16)
-            interleave(on_vector, bf[:], xm_raw[:, :, block[m]])
+            interleave(on_vector, bf[:], xm_block[m])
             return bf
 
         def quantize_xm(bf, m):
@@ -196,8 +200,9 @@ def tile_attend_ghv_lch_kernel(tc, xT, wT, vT, y, wt, xm, offs, out):
                 in_=bf[:].rearrange("p c t -> p (c t)"),
             )
 
-        xm_bf0 = round_xm(False, "staging", 0)
+        xm_bf0 = round_xm(False, "xm_bf0", 0)
         xm_bf1 = round_xm(False, "xm_bf1", 1)
+        quantize_xm(xm_bf0, 0)
 
         g_bf = sb("g_bf", [P, N - Q, PACK], BF16)
         g_last = sb("g_last", [P, Q, PACK], BF16)
@@ -236,7 +241,6 @@ def tile_attend_ghv_lch_kernel(tc, xT, wT, vT, y, wt, xm, offs, out):
         for n in range(QUARTERS - 1):
             form_g(n, g_bf[:, quarter[n], :])
         quantize_g(0, HALF, g_bf[:, half[0], :])
-        quantize_xm(xm_bf0, 0)
         quantize_g(HALF, N - Q, g_bf[:, quarter[2], :])
         first = product("bank0", 0, 0)
         nc.scalar.copy(out=dense[0][:, 0 : N - Q], in_=first[:, Q:N])
@@ -244,10 +248,10 @@ def tile_attend_ghv_lch_kernel(tc, xT, wT, vT, y, wt, xm, offs, out):
         quantize_xm(xm_bf1, 1)
         quantize_g(N - Q, N, g_last[:])
         second = product("bank1", 0, Q)
-        nc.scalar.copy(out=dense[0][:, quarter[3]], in_=second[:, quarter[3]])
         xm_bf2 = round_xm(True, "g_last", 2)
         split = (N - Q) // PER_COLUMN
         nc.vector.tensor_copy(wide[0][:].indirect(offsets[:, 0:split]), dense[0][:, 0 : N - Q])
+        nc.vector.tensor_copy(out=dense[0][:, quarter[3]], in_=second[:, quarter[3]])
         nc.vector.tensor_tensor(
             out=wide[0][:].indirect(offsets[:, split : N // PER_COLUMN]),
             in0=dense[0][:, quarter[3]],

@@ -40,11 +40,11 @@ def tile_attend_ghv_lch_kernel(tc, xT, wT, vT, y, wt, xm, offs, out):
         offsets = keep.tile([P, N // PER_COLUMN], U16, name="offsets")
         half_offsets = [offsets[:, 0 : HALF // PER_COLUMN], offsets[:, HALF // PER_COLUMN : N // PER_COLUMN]]
         x_raw = sb("x_raw", [P, PACK, R], F32)
-        w_pair = sb("w_pair", [P, 2, T], F32)
-        w_late = [sb(f"w_late{u}", [P, T], F32) for u in range(2)]
+        w_early = sb("w_early", [P, PACK - 1, T], F32)
+        w_last = sb("w_last", [P, T], F32)
         v_pair = sb("v_pair", [P, 2, T], F32)
         v_late = [sb(f"v_late{u}", [P, T], F32) for u in range(2)]
-        w_plane = [w_pair[:, 0, :], w_pair[:, 1, :], w_late[0][:], w_late[1][:]]
+        w_plane = [w_early[:, t, :] for t in range(PACK - 1)] + [w_last[:]]
         v_plane = [v_pair[:, 0, :], v_pair[:, 1, :], v_late[0][:], v_late[1][:]]
         y_sb = sb("y_sb", [P, PACK, N], F32)
         wt_sb = sb("wt_sb", [P, PACK], F32)
@@ -54,13 +54,12 @@ def tile_attend_ghv_lch_kernel(tc, xT, wT, vT, y, wt, xm, offs, out):
 
         w_rows = wT.rearrange("(p t) c -> p t c", t=PACK)
         v_rows = vT.rearrange("(p t) c -> p t c", t=PACK)
+        nc.scalar.dma_start(out=wt_sb[:], in_=wt.rearrange("b (p t) o -> p (b t o)", t=PACK))
         nc.sync.dma_start(out=x_raw[:], in_=xT.rearrange("b (p t) r -> p (b t) r", t=PACK))
         nc.sync.dma_start(offsets[:], offs)
-        nc.sync.dma_start(out=w_pair[:], in_=w_rows[:, 0:2, :])
-        for u in range(2):
-            nc.sync.dma_start(out=w_late[u][:], in_=w_rows[:, 2 + u, :])
+        nc.sync.dma_start(out=w_early[:], in_=w_rows[:, 0 : PACK - 1, :])
+        nc.sync.dma_start(out=w_last[:], in_=w_rows[:, PACK - 1, :])
         nc.sync.dma_start(out=y_sb[:], in_=y.rearrange("b (p t) i -> p (b t) i", t=PACK))
-        nc.sync.dma_start(out=wt_sb[:], in_=wt.rearrange("b (p t) o -> p (b t o)", t=PACK))
         nc.sync.dma_start(out=v_pair[:], in_=v_rows[:, 0:2, :])
         for u in range(2):
             nc.sync.dma_start(out=v_late[u][:], in_=v_rows[:, 2 + u, :])

@@ -8,6 +8,7 @@ FLOPS = 3 * 2 * D * R * N
 F32 = mybir.dt.float32
 BF16 = mybir.dt.bfloat16
 U32 = mybir.dt.uint32
+I32 = mybir.dt.int32
 U16 = mybir.dt.uint16
 U8 = mybir.dt.uint8
 E4M3 = mybir.dt.float8_e4m3fn_x4
@@ -22,6 +23,8 @@ Q = N // QUARTERS
 HALF = N // 2
 PER_COLUMN = 16
 BLOCKS = D // P
+WARM_ROWS = 32
+WARM_RUN = 5
 
 
 def tile_attend_ghv_lch_kernel(tc, xT, wT, vT, y, wt, xm, offs, out):
@@ -180,6 +183,23 @@ def tile_attend_ghv_lch_kernel(tc, xT, wT, vT, y, wt, xm, offs, out):
             form_h(t)
             gather_v(t)
         form_h(QUARTERS - 1)
+
+        def warm_up(bank_name, codes, passes):
+            bank = psum.tile([P, N], F32, name=bank_name)
+            for i in range(passes):
+                nc.tensor.matmul_mx(
+                    out=bank[0:WARM_ROWS, :],
+                    lhsT=codes.bitcast(E4M3),
+                    lhsT_scale=x_scales[:, 0:WARM_ROWS],
+                    rhs=w_codes[:].bitcast(E4M3),
+                    rhs_scale=w_scales[:],
+                    start=True,
+                    stop=True,
+                )
+
+        warm_codes = sb("v_late0", [P, WARM_ROWS], U32)
+        nc.vector.tensor_copy(out=warm_codes[:].bitcast(I32), in_=x_codes[:, 0:WARM_ROWS].bitcast(I32))
+        warm_up("bank3", warm_codes[:], WARM_RUN)
         for u in range(2):
             nc.vector.tensor_copy(v_got[:, PACK - 1, half[u]], v_plane[PACK - 1].indirect(half_offsets[u]))
         prepare(v_codes, v_scales, v_bf, v_got)
@@ -239,6 +259,8 @@ def tile_attend_ghv_lch_kernel(tc, xT, wT, vT, y, wt, xm, offs, out):
 
         for n in range(QUARTERS - 1):
             form_g(n, g_bf[:, quarter[n], :])
+        for n in range(QUARTERS - 1):
+            warm_up(f"bank{QUARTERS + n}", warm_codes[:], 1)
         quantize_g(0, HALF, g_bf[:, half[0], :])
         quantize_g(HALF, N - Q, g_bf[:, quarter[2], :])
         first = product("bank0", 0, 0)

@@ -24,7 +24,6 @@ HALF = N // 2
 PER_COLUMN = 16
 BLOCKS = D // P
 WARM_ROWS = 32
-WARM_RUN = 5
 
 
 def tile_attend_ghv_lch_kernel(tc, xT, wT, vT, y, wt, xm, offs, out):
@@ -184,22 +183,22 @@ def tile_attend_ghv_lch_kernel(tc, xT, wT, vT, y, wt, xm, offs, out):
             gather_v(t)
         form_h(QUARTERS - 1)
 
-        def warm_up(bank_name, codes, passes):
+        def warm_up(bank_name, codes):
             bank = psum.tile([P, N], F32, name=bank_name)
-            for i in range(passes):
-                nc.tensor.matmul_mx(
-                    out=bank[0:WARM_ROWS, :],
-                    lhsT=codes.bitcast(E4M3),
-                    lhsT_scale=x_scales[:, 0:WARM_ROWS],
-                    rhs=w_codes[:].bitcast(E4M3),
-                    rhs_scale=w_scales[:],
-                    start=True,
-                    stop=True,
-                )
+            nc.tensor.matmul_mx(
+                out=bank[0:WARM_ROWS, :],
+                lhsT=codes.bitcast(E4M3),
+                lhsT_scale=x_scales[:, 0:WARM_ROWS],
+                rhs=w_codes[:].bitcast(E4M3),
+                rhs_scale=w_scales[:],
+                start=True,
+                stop=True,
+            )
 
         warm_codes = sb("v_late0", [P, WARM_ROWS], U32)
         nc.vector.tensor_copy(out=warm_codes[:].bitcast(I32), in_=x_codes[:, 0:WARM_ROWS].bitcast(I32))
-        warm_up("bank3", warm_codes[:], WARM_RUN)
+        for n in range(QUARTERS):
+            warm_up(f"bank{n}", warm_codes[:])
         for u in range(2):
             nc.vector.tensor_copy(v_got[:, PACK - 1, half[u]], v_plane[PACK - 1].indirect(half_offsets[u]))
         prepare(v_codes, v_scales, v_bf, v_got)
@@ -260,7 +259,7 @@ def tile_attend_ghv_lch_kernel(tc, xT, wT, vT, y, wt, xm, offs, out):
         for n in range(QUARTERS - 1):
             form_g(n, g_bf[:, quarter[n], :])
         for n in range(QUARTERS - 1):
-            warm_up(f"bank{QUARTERS + n}", warm_codes[:], 1)
+            warm_up(f"bank{QUARTERS + n}", warm_codes[:])
         quantize_g(0, HALF, g_bf[:, half[0], :])
         quantize_g(HALF, N - Q, g_bf[:, quarter[2], :])
         first = product("bank0", 0, 0)

@@ -195,10 +195,10 @@ def tile_attend_ghv_lch_kernel(tc, xT, wT, vT, y, wt, xm, offs, out):
                 stop=True,
             )
 
-        warm_codes = sb("v_late0", [P, WARM_ROWS], U32)
+        warm_codes = sb("v_pair", [P, WARM_ROWS], U32)
         nc.vector.tensor_copy(out=warm_codes[:].bitcast(I32), in_=x_codes[:, 0:WARM_ROWS].bitcast(I32))
-        for n in range(QUARTERS):
-            warm_up(f"bank{n}", warm_codes[:])
+        for n in range(QUARTERS + 1):
+            warm_up(f"bank{n % QUARTERS}", warm_codes[:])
         for u in range(2):
             nc.vector.tensor_copy(v_got[:, PACK - 1, half[u]], v_plane[PACK - 1].indirect(half_offsets[u]))
         prepare(v_codes, v_scales, v_bf, v_got)

@@ -30,6 +30,7 @@ def tile_attend_ghv_lch_kernel(tc, xT, wT, vT, y, wt, xm, offs, out):
     nc = tc.nc
     with ExitStack() as ctx:
         keep = ctx.enter_context(tc.tile_pool(name="keep", bufs=1))
+        shared = ctx.enter_context(tc.tile_pool(name="shared", bufs=1))
         psum = ctx.enter_context(tc.psum_pool(name="psum", bufs=1))
 
         def sb(name, shape, dtype):
@@ -44,7 +45,7 @@ def tile_attend_ghv_lch_kernel(tc, xT, wT, vT, y, wt, xm, offs, out):
         x_raw = sb("x_raw", [P, PACK, R], F32)
         w_early = sb("w_early", [P, PACK - 1, T], F32)
         w_last = sb("w_last", [P, T], F32)
-        v_pair = sb("v_pair", [P, 2, T], F32)
+        v_pair = shared.tile([P, 2, T], F32, name="v_pair", align_bytes=64, offset=0)
         v_late = [sb(f"v_late{u}", [P, T], F32) for u in range(2)]
         w_plane = [w_early[:, t, :] for t in range(PACK - 1)] + [w_last[:]]
         v_plane = [v_pair[:, 0, :], v_pair[:, 1, :], v_late[0][:], v_late[1][:]]
@@ -139,7 +140,9 @@ def tile_attend_ghv_lch_kernel(tc, xT, wT, vT, y, wt, xm, offs, out):
         z = sb("z", [P, N, PACK], F32)
         q = sb("q", [P, N, PACK], F32)
         q2 = sb("q2", [P, N, PACK], F32)
-        h = sb("h", [P, N, PACK], F32)
+        h = [sb(f"h{n}", [P, Q, PACK], F32) for n in range(2)]
+        h.append(shared.tile([P, Q, PACK], F32, name="h2", align_bytes=64, offset=0))
+        h.append(sb("h3", [P, Q, PACK], F32))
 
         def square(n):
             nc.scalar.activation(out=q2[:, quarter[n], :], in_=q[:, quarter[n], :], func=ACT.Square)
@@ -162,7 +165,7 @@ def tile_attend_ghv_lch_kernel(tc, xT, wT, vT, y, wt, xm, offs, out):
 
         def form_h(n):
             nc.vector.scalar_tensor_tensor(
-                out=h[:, quarter[n], :],
+                out=h[n][:],
                 in0=q2[:, quarter[n], :],
                 scalar=1.0,
                 in1=neg_wt[:].unsqueeze(1).to_broadcast([P, Q, PACK]),
@@ -178,11 +181,6 @@ def tile_attend_ghv_lch_kernel(tc, xT, wT, vT, y, wt, xm, offs, out):
         def gather_v(t):
             nc.vector.tensor_copy(v_got[:, t, :], v_plane[t].indirect(offsets[:]))
 
-        for t in range(PACK - 1):
-            form_h(t)
-            gather_v(t)
-        form_h(QUARTERS - 1)
-
         def warm_up(bank_name, codes):
             bank = psum.tile([P, N], F32, name=bank_name)
             nc.tensor.matmul_mx(
@@ -195,10 +193,16 @@ def tile_attend_ghv_lch_kernel(tc, xT, wT, vT, y, wt, xm, offs, out):
                 stop=True,
             )
 
-        warm_codes = sb("v_pair", [P, WARM_ROWS], U32)
+        for t in range(2):
+            form_h(t)
+            gather_v(t)
+        warm_codes = shared.tile([P, WARM_ROWS], U32, name="warm_codes", align_bytes=64, offset=Q * PACK * 4)
         nc.vector.tensor_copy(out=warm_codes[:].bitcast(I32), in_=x_codes[:, 0:WARM_ROWS].bitcast(I32))
         for n in range(QUARTERS + 1):
             warm_up(f"bank{n % QUARTERS}", warm_codes[:])
+        form_h(2)
+        gather_v(2)
+        form_h(3)
         for u in range(2):
             nc.vector.tensor_copy(v_got[:, PACK - 1, half[u]], v_plane[PACK - 1].indirect(half_offsets[u]))
         prepare(v_codes, v_scales, v_bf, v_got)
@@ -230,7 +234,7 @@ def tile_attend_ghv_lch_kernel(tc, xT, wT, vT, y, wt, xm, offs, out):
             nc.vector.tensor_tensor(
                 out=dst,
                 in0=av[:].rearrange("p t i -> p i t"),
-                in1=h[:, quarter[n], :],
+                in1=h[n][:],
                 op=ALU.mult,
             )
 

@@ -229,14 +229,16 @@ def tile_attend_ghv_lch_kernel(tc, xT, wT, vT, y, wt, xm, offs, out):
         g_bf = sb("g_bf", [P, N - Q, PACK], BF16)
         g_last = sb("g_last", [P, Q, PACK], BF16)
 
-        def form_g(n, dst):
+        def form_g(n, dst, pieces=1):
             av = scores(f"bank{QUARTERS + n}", v_codes, v_scales, n)
-            nc.vector.tensor_tensor(
-                out=dst,
-                in0=av[:].rearrange("p t i -> p i t"),
-                in1=h[n][:],
-                op=ALU.mult,
-            )
+            for u in range(pieces):
+                cols = slice(u * Q // pieces, (u + 1) * Q // pieces)
+                nc.vector.tensor_tensor(
+                    out=dst[:, cols, :],
+                    in0=av[:, :, cols].rearrange("p t i -> p i t"),
+                    in1=h[n][:, cols, :],
+                    op=ALU.mult,
+                )
 
         def quantize_g(first, last, src):
             nc.vector.quantize_mx(
@@ -268,9 +270,10 @@ def tile_attend_ghv_lch_kernel(tc, xT, wT, vT, y, wt, xm, offs, out):
         quantize_g(HALF, N - Q, g_bf[:, quarter[2], :])
         first = product("bank0", 0, 0)
         nc.scalar.copy(out=dense[0][:, 0 : N - Q], in_=first[:, Q:N])
-        form_g(QUARTERS - 1, g_last[:])
+        form_g(QUARTERS - 1, g_last[:], 2)
+        quantize_g(N - Q, N - Q // 2, g_last[:, 0 : Q // 2, :])
+        quantize_g(N - Q // 2, N, g_last[:, Q // 2 : Q, :])
         quantize_xm(xm_bf1, 1)
-        quantize_g(N - Q, N, g_last[:])
         second = product("bank1", 0, Q)
         xm_bf2 = round_xm(True, "g_last", 2)
         split = (N - Q) // PER_COLUMN

@@ -278,7 +278,7 @@ def tile_attend_ghv_lch_kernel(tc, xT, wT, vT, y, wt, xm, offs, out):
         xm_bf2 = round_xm(True, "g_last", 2)
         split = (N - Q) // PER_COLUMN
         nc.vector.tensor_copy(wide[0][:].indirect(offsets[:, 0:split]), dense[0][:, 0 : N - Q])
-        nc.vector.tensor_copy(out=dense[0][:, quarter[3]], in_=second[:, quarter[3]])
+        nc.scalar.copy(out=dense[0][:, quarter[3]], in_=second[:, quarter[3]])
         nc.vector.tensor_tensor(
             out=wide[0][:].indirect(offsets[:, split : N // PER_COLUMN]),
             in0=dense[0][:, quarter[3]],

@@ -77,7 +77,7 @@ def tile_attend_ghv_lch_kernel(tc, xT, wT, vT, y, wt, xm, offs, out):
         g_scales = sb("g_scales", [P, Q + N], U8)
         nc.vector.memset(g_codes[:, 0:Q], 0)
         nc.vector.memset(g_scales[:, 0:Q].bitcast(U32), 0)
-        zeros = sb("zeros", [P, Q], F32)
+        zeros = shared.tile([P, Q], F32, name="zeros", align_bytes=64, offset=2 * T * 4)
         nc.vector.memset(zeros[:], 0.0)
 
         x_bf = sb("x_bf", [P, R * PACK], BF16)
@@ -207,7 +207,9 @@ def tile_attend_ghv_lch_kernel(tc, xT, wT, vT, y, wt, xm, offs, out):
             nc.vector.tensor_copy(v_got[:, PACK - 1, half[u]], v_plane[PACK - 1].indirect(half_offsets[u]))
         prepare(v_codes, v_scales, v_bf, v_got)
 
-        xm_codes = sb("xm_codes", [P, D], U32)
+        xm_codes = [sb(f"xm_codes{m}", [P, P], U32) for m in range(2)]
+        xm_codes.append(shared.tile([P, P], U32, name="xm_codes2", align_bytes=64, offset=2 * Q * PACK * 4))
+        xm_codes.append(shared.tile([P, P], U32, name="xm_codes3", align_bytes=64, offset=2 * T * 4))
         xm_scales = sb("xm_scales", [P, D], U8)
 
         def round_xm(on_vector, tile_name, m):
@@ -217,17 +219,19 @@ def tile_attend_ghv_lch_kernel(tc, xT, wT, vT, y, wt, xm, offs, out):
 
         def quantize_xm(bf, m):
             nc.vector.quantize_mx(
-                out=xm_codes[:, block[m]].bitcast(E4M3),
+                out=xm_codes[m][:].bitcast(E4M3),
                 scales=xm_scales[:, block[m]],
                 in_=bf[:].rearrange("p c t -> p (c t)"),
             )
 
         xm_bf0 = round_xm(False, "xm_bf0", 0)
         xm_bf1 = round_xm(False, "xm_bf1", 1)
+        xm_bf2 = round_xm(False, "xm_bf2", 2)
+        xm_bf3 = round_xm(False, "xm_bf3", 3)
         quantize_xm(xm_bf0, 0)
 
         g_bf = sb("g_bf", [P, N - Q, PACK], BF16)
-        g_last = sb("g_last", [P, Q, PACK], BF16)
+        g_last = shared.tile([P, Q, PACK], BF16, name="g_last", align_bytes=64, offset=2 * Q * PACK * 4)
 
         def form_g(n, dst, pieces=1):
             av = scores(f"bank{QUARTERS + n}", v_codes, v_scales, n)
@@ -251,7 +255,7 @@ def tile_attend_ghv_lch_kernel(tc, xT, wT, vT, y, wt, xm, offs, out):
             dw = psum.tile([P, N], F32, name=bank_name)
             nc.tensor.matmul_mx(
                 out=dw[:],
-                lhsT=xm_codes[:, block[m]].bitcast(E4M3),
+                lhsT=xm_codes[m][:].bitcast(E4M3),
                 lhsT_scale=xm_scales[:, block[m]],
                 rhs=g_codes[:, first_col : first_col + N].bitcast(E5M2),
                 rhs_scale=g_scales[:, first_col : first_col + N],
@@ -275,7 +279,7 @@ def tile_attend_ghv_lch_kernel(tc, xT, wT, vT, y, wt, xm, offs, out):
         quantize_g(N - Q // 2, N, g_last[:, Q // 2 : Q, :])
         quantize_xm(xm_bf1, 1)
         second = product("bank1", 0, Q)
-        xm_bf2 = round_xm(True, "g_last", 2)
+        quantize_xm(xm_bf2, 2)
         split = (N - Q) // PER_COLUMN
         nc.vector.tensor_copy(wide[0][:].indirect(offsets[:, 0:split]), dense[0][:, 0 : N - Q])
         nc.scalar.copy(out=dense[0][:, quarter[3]], in_=second[:, quarter[3]])
@@ -286,7 +290,7 @@ def tile_attend_ghv_lch_kernel(tc, xT, wT, vT, y, wt, xm, offs, out):
             op=ALU.add,
         )
         nc.sync.dma_start(out=out[block[0], :], in_=wide[0][:])
-        quantize_xm(xm_bf2, 2)
+        quantize_xm(xm_bf3, 3)
 
         def finish(m):
             dw = product(f"bank{(m + 1) % QUARTERS}", m, Q)
@@ -294,8 +298,5 @@ def tile_attend_ghv_lch_kernel(tc, xT, wT, vT, y, wt, xm, offs, out):
             nc.vector.tensor_copy(wide[m][:].indirect(offsets[:]), dense[m][:])
             nc.sync.dma_start(out=out[block[m], :], in_=wide[m][:])
 
-        finish(1)
-        xm_bf3 = round_xm(True, "dense0", 3)
-        finish(2)
-        quantize_xm(xm_bf3, 3)
-        finish(3)
+        for m in range(1, BLOCKS):
+            finish(m)

@@ -73,10 +73,10 @@ def tile_attend_ghv_lch_kernel(tc, xT, wT, vT, y, wt, xm, offs, out):
         wide = [sb(f"wide{m}", [P, T], F32) for m in range(BLOCKS)]
         for m in range(BLOCKS):
             nc.vector.memset(wide[m][:].bitcast(U32), 0)
-        g_codes = sb("g_codes", [P, Q + N], U32)
-        g_scales = sb("g_scales", [P, Q + N], U8)
-        nc.vector.memset(g_codes[:, 0:Q], 0)
-        nc.vector.memset(g_scales[:, 0:Q].bitcast(U32), 0)
+        g_codes = sb("g_codes", [P, HALF + N], U32)
+        g_scales = sb("g_scales", [P, HALF + N], U8)
+        nc.vector.memset(g_codes[:, 0:HALF], 0)
+        nc.vector.memset(g_scales[:, 0:HALF].bitcast(U32), 0)
         zeros = shared.tile([P, Q], F32, name="zeros", align_bytes=64, offset=2 * T * 4)
         nc.vector.memset(zeros[:], 0.0)
 
@@ -139,13 +139,14 @@ def tile_attend_ghv_lch_kernel(tc, xT, wT, vT, y, wt, xm, offs, out):
 
         z = sb("z", [P, N, PACK], F32)
         q = sb("q", [P, N, PACK], F32)
-        q2 = sb("q2", [P, N, PACK], F32)
+        q2 = [sb(f"q2_{n}", [P, Q, PACK], F32) for n in range(QUARTERS - 1)]
+        q2.append(shared.tile([P, Q, PACK], F32, name="q2_3", align_bytes=64, offset=2 * T * 4 + Q * 4))
         h = [sb(f"h{n}", [P, Q, PACK], F32) for n in range(2)]
         h.append(shared.tile([P, Q, PACK], F32, name="h2", align_bytes=64, offset=0))
         h.append(sb("h3", [P, Q, PACK], F32))
 
         def square(n):
-            nc.scalar.activation(out=q2[:, quarter[n], :], in_=q[:, quarter[n], :], func=ACT.Square)
+            nc.scalar.activation(out=q2[n][:], in_=q[:, quarter[n], :], func=ACT.Square)
 
         for n in range(QUARTERS):
             a = scores(f"bank{n}", w_codes, w_scales, n)
@@ -166,7 +167,7 @@ def tile_attend_ghv_lch_kernel(tc, xT, wT, vT, y, wt, xm, offs, out):
         def form_h(n):
             nc.vector.scalar_tensor_tensor(
                 out=h[n][:],
-                in0=q2[:, quarter[n], :],
+                in0=q2[n][:],
                 scalar=1.0,
                 in1=neg_wt[:].unsqueeze(1).to_broadcast([P, Q, PACK]),
                 op0=ALU.subtract,
@@ -196,13 +197,13 @@ def tile_attend_ghv_lch_kernel(tc, xT, wT, vT, y, wt, xm, offs, out):
         for t in range(2):
             form_h(t)
             gather_v(t)
-        warm_codes = shared.tile([P, WARM_ROWS], U32, name="warm_codes", align_bytes=64, offset=Q * PACK * 4)
-        nc.vector.tensor_copy(out=warm_codes[:].bitcast(I32), in_=x_codes[:, 0:WARM_ROWS].bitcast(I32))
-        for n in range(QUARTERS + 1):
-            warm_up(f"bank{n % QUARTERS}", warm_codes[:])
         form_h(2)
-        gather_v(2)
         form_h(3)
+        warm_codes = shared.tile([P, WARM_ROWS], U32, name="warm_codes", align_bytes=64, offset=2 * T * 4 + Q * 4)
+        nc.vector.tensor_copy(out=warm_codes[:].bitcast(I32), in_=x_codes[:, 0:WARM_ROWS].bitcast(I32))
+        for n in range(3):
+            warm_up(f"bank{n}", warm_codes[:])
+        gather_v(2)
         for u in range(2):
             nc.vector.tensor_copy(v_got[:, PACK - 1, half[u]], v_plane[PACK - 1].indirect(half_offsets[u]))
         prepare(v_codes, v_scales, v_bf, v_got)
@@ -234,7 +235,7 @@ def tile_attend_ghv_lch_kernel(tc, xT, wT, vT, y, wt, xm, offs, out):
         g_last = shared.tile([P, Q, PACK], BF16, name="g_last", align_bytes=64, offset=2 * Q * PACK * 4)
 
         def form_g(n, dst, pieces=1):
-            av = scores(f"bank{QUARTERS + n}", v_codes, v_scales, n)
+            av = scores(f"bank{QUARTERS + (n if n < 3 else 1)}", v_codes, v_scales, n)
             for u in range(pieces):
                 cols = slice(u * Q // pieces, (u + 1) * Q // pieces)
                 nc.vector.tensor_tensor(
@@ -246,8 +247,8 @@ def tile_attend_ghv_lch_kernel(tc, xT, wT, vT, y, wt, xm, offs, out):
 
         def quantize_g(first, last, src):
             nc.vector.quantize_mx(
-                out=g_codes[:, Q + first : Q + last].bitcast(E5M2),
-                scales=g_scales[:, Q + first : Q + last],
+                out=g_codes[:, HALF + first : HALF + last].bitcast(E5M2),
+                scales=g_scales[:, HALF + first : HALF + last],
                 in_=src.rearrange("p i t -> p (i t)"),
             )
 
@@ -268,20 +269,26 @@ def tile_attend_ghv_lch_kernel(tc, xT, wT, vT, y, wt, xm, offs, out):
 
         for n in range(QUARTERS - 1):
             form_g(n, g_bf[:, quarter[n], :])
-        for n in range(QUARTERS - 1):
-            warm_up(f"bank{QUARTERS + n}", warm_codes[:])
         quantize_g(0, HALF, g_bf[:, half[0], :])
+        early = product("bank7", 0, 0)
+        nc.scalar.copy(out=dense[0][:, half[0]], in_=early[:, half[1]])
         quantize_g(HALF, N - Q, g_bf[:, quarter[2], :])
-        first = product("bank0", 0, 0)
-        nc.scalar.copy(out=dense[0][:, 0 : N - Q], in_=first[:, Q:N])
+        first = product("bank0", 0, Q)
+        nc.scalar.copy(out=dense[0][:, quarter[2]], in_=first[:, quarter[3]])
         form_g(QUARTERS - 1, g_last[:], 2)
         quantize_g(N - Q, N - Q // 2, g_last[:, 0 : Q // 2, :])
         quantize_g(N - Q // 2, N, g_last[:, Q // 2 : Q, :])
         quantize_xm(xm_bf1, 1)
-        second = product("bank1", 0, Q)
+        second = product("bank1", 0, HALF)
         quantize_xm(xm_bf2, 2)
         split = (N - Q) // PER_COLUMN
-        nc.vector.tensor_copy(wide[0][:].indirect(offsets[:, 0:split]), dense[0][:, 0 : N - Q])
+        nc.vector.tensor_copy(wide[0][:].indirect(half_offsets[0]), dense[0][:, half[0]])
+        nc.vector.tensor_tensor(
+            out=wide[0][:].indirect(offsets[:, HALF // PER_COLUMN : split]),
+            in0=dense[0][:, quarter[2]],
+            in1=zeros[:],
+            op=ALU.add,
+        )
         nc.scalar.copy(out=dense[0][:, quarter[3]], in_=second[:, quarter[3]])
         nc.vector.tensor_tensor(
             out=wide[0][:].indirect(offsets[:, split : N // PER_COLUMN]),
@@ -293,7 +300,7 @@ def tile_attend_ghv_lch_kernel(tc, xT, wT, vT, y, wt, xm, offs, out):
         quantize_xm(xm_bf3, 3)
 
         def finish(m):
-            dw = product(f"bank{(m + 1) % QUARTERS}", m, Q)
+            dw = product(f"bank{(m + 1) % QUARTERS}", m, HALF)
             nc.scalar.copy(out=dense[m][:], in_=dw[:])
             nc.vector.tensor_copy(wide[m][:].indirect(offsets[:]), dense[m][:])
             nc.sync.dma_start(out=out[block[m], :], in_=wide[m][:])

@@ -235,7 +235,7 @@ def tile_attend_ghv_lch_kernel(tc, xT, wT, vT, y, wt, xm, offs, out):
         g_last = shared.tile([P, Q, PACK], BF16, name="g_last", align_bytes=64, offset=2 * Q * PACK * 4)
 
         def form_g(n, dst, pieces=1):
-            av = scores(f"bank{QUARTERS + (n if n < 3 else 1)}", v_codes, v_scales, n)
+            av = scores(f"bank{QUARTERS + n}", v_codes, v_scales, n)
             for u in range(pieces):
                 cols = slice(u * Q // pieces, (u + 1) * Q // pieces)
                 nc.vector.tensor_tensor(
@@ -270,7 +270,7 @@ def tile_attend_ghv_lch_kernel(tc, xT, wT, vT, y, wt, xm, offs, out):
         for n in range(QUARTERS - 1):
             form_g(n, g_bf[:, quarter[n], :])
         quantize_g(0, HALF, g_bf[:, half[0], :])
-        early = product("bank7", 0, 0)
+        early = product("bank3", 0, 0)
         nc.scalar.copy(out=dense[0][:, half[0]], in_=early[:, half[1]])
         quantize_g(HALF, N - Q, g_bf[:, quarter[2], :])
         first = product("bank0", 0, Q)

@@ -209,8 +209,8 @@ def tile_attend_ghv_lch_kernel(tc, xT, wT, vT, y, wt, xm, offs, out):
         prepare(v_codes, v_scales, v_bf, v_got)
 
         xm_codes = [sb(f"xm_codes{m}", [P, P], U32) for m in range(2)]
-        xm_codes.append(shared.tile([P, P], U32, name="xm_codes2", align_bytes=64, offset=2 * Q * PACK * 4))
-        xm_codes.append(shared.tile([P, P], U32, name="xm_codes3", align_bytes=64, offset=2 * T * 4))
+        xm_codes.append(shared.tile([P, P], U32, name="xm_codes2", align_bytes=64, offset=2 * T * 4 - P * 2))
+        xm_codes.append(shared.tile([P, P], U32, name="xm_codes3", align_bytes=64, offset=2 * T * 4 + P * 2))
         xm_scales = sb("xm_scales", [P, D], U8)
 
         def round_xm(on_vector, tile_name, m):
@@ -232,7 +232,7 @@ def tile_attend_ghv_lch_kernel(tc, xT, wT, vT, y, wt, xm, offs, out):
         quantize_xm(xm_bf0, 0)
 
         g_bf = sb("g_bf", [P, N - Q, PACK], BF16)
-        g_last = shared.tile([P, Q, PACK], BF16, name="g_last", align_bytes=64, offset=2 * Q * PACK * 4)
+        g_last = sb("g_last", [P, Q, PACK], BF16)
 
         def form_g(n, dst, pieces=1):
             av = scores(f"bank{QUARTERS + n}", v_codes, v_scales, n)
@@ -280,15 +280,8 @@ def tile_attend_ghv_lch_kernel(tc, xT, wT, vT, y, wt, xm, offs, out):
         quantize_g(N - Q // 2, N, g_last[:, Q // 2 : Q, :])
         quantize_xm(xm_bf1, 1)
         second = product("bank1", 0, HALF)
-        quantize_xm(xm_bf2, 2)
         split = (N - Q) // PER_COLUMN
-        nc.vector.tensor_copy(wide[0][:].indirect(half_offsets[0]), dense[0][:, half[0]])
-        nc.vector.tensor_tensor(
-            out=wide[0][:].indirect(offsets[:, HALF // PER_COLUMN : split]),
-            in0=dense[0][:, quarter[2]],
-            in1=zeros[:],
-            op=ALU.add,
-        )
+        nc.vector.tensor_copy(wide[0][:].indirect(offsets[:, 0:split]), dense[0][:, 0 : N - Q])
         nc.scalar.copy(out=dense[0][:, quarter[3]], in_=second[:, quarter[3]])
         nc.vector.tensor_tensor(
             out=wide[0][:].indirect(offsets[:, split : N // PER_COLUMN]),
@@ -297,6 +290,7 @@ def tile_attend_ghv_lch_kernel(tc, xT, wT, vT, y, wt, xm, offs, out):
             op=ALU.add,
         )
         nc.sync.dma_start(out=out[block[0], :], in_=wide[0][:])
+        quantize_xm(xm_bf2, 2)
         quantize_xm(xm_bf3, 3)
 
         def finish(m):

@@ -214,7 +214,10 @@ def tile_attend_ghv_lch_kernel(tc, xT, wT, vT, y, wt, xm, offs, out):
         xm_scales = sb("xm_scales", [P, D], U8)
 
         def round_xm(on_vector, tile_name, m):
-            bf = sb(tile_name, [P, P, PACK], BF16)
+            if m == BLOCKS - 1:
+                bf = shared.tile([P, P, PACK], BF16, name=tile_name, align_bytes=64, offset=3 * T * 4)
+            else:
+                bf = sb(tile_name, [P, P, PACK], BF16)
             interleave(on_vector, bf[:], xm_block[m])
             return bf
 
@@ -228,7 +231,6 @@ def tile_attend_ghv_lch_kernel(tc, xT, wT, vT, y, wt, xm, offs, out):
         xm_bf0 = round_xm(False, "xm_bf0", 0)
         xm_bf1 = round_xm(False, "xm_bf1", 1)
         xm_bf2 = round_xm(False, "xm_bf2", 2)
-        xm_bf3 = round_xm(False, "xm_bf3", 3)
         quantize_xm(xm_bf0, 0)
 
         g_bf = sb("g_bf", [P, N - Q, PACK], BF16)
@@ -265,7 +267,8 @@ def tile_attend_ghv_lch_kernel(tc, xT, wT, vT, y, wt, xm, offs, out):
             )
             return dw
 
-        dense = [sb(f"dense{m}", [P, N], F32) for m in range(BLOCKS)]
+        dense = [shared.tile([P, N], F32, name="dense0", align_bytes=64, offset=3 * T * 4)]
+        dense.extend(sb(f"dense{m}", [P, N], F32) for m in range(1, BLOCKS))
 
         for n in range(QUARTERS - 1):
             form_g(n, g_bf[:, quarter[n], :])
@@ -291,6 +294,7 @@ def tile_attend_ghv_lch_kernel(tc, xT, wT, vT, y, wt, xm, offs, out):
         )
         nc.sync.dma_start(out=out[block[0], :], in_=wide[0][:])
         quantize_xm(xm_bf2, 2)
+        xm_bf3 = round_xm(False, "xm_bf3", 3)
         quantize_xm(xm_bf3, 3)
 
         def finish(m):

@@ -34,7 +34,7 @@ def tile_attend_ghv_lch_kernel(tc, xT, wT, vT, y, wt, xm, offs, out):
         psum = ctx.enter_context(tc.psum_pool(name="psum", bufs=1))
 
         def sb(name, shape, dtype):
-            return keep.tile(shape, dtype, name=name, align_bytes=64)
+            return keep.tile(shape, dtype, name=name, align_bytes=256)
 
         quarter = [slice(n * Q, (n + 1) * Q) for n in range(QUARTERS)]
         half = [slice(0, HALF), slice(HALF, N)]
@@ -45,7 +45,7 @@ def tile_attend_ghv_lch_kernel(tc, xT, wT, vT, y, wt, xm, offs, out):
         x_raw = sb("x_raw", [P, PACK, R], F32)
         w_early = sb("w_early", [P, PACK - 1, T], F32)
         w_last = sb("w_last", [P, T], F32)
-        v_pair = shared.tile([P, 2, T], F32, name="v_pair", align_bytes=64, offset=0)
+        v_pair = shared.tile([P, 2, T], F32, name="v_pair", align_bytes=256, offset=0)
         v_late = [sb(f"v_late{u}", [P, T], F32) for u in range(2)]
         w_plane = [w_early[:, t, :] for t in range(PACK - 1)] + [w_last[:]]
         v_plane = [v_pair[:, 0, :], v_pair[:, 1, :], v_late[0][:], v_late[1][:]]
@@ -77,7 +77,7 @@ def tile_attend_ghv_lch_kernel(tc, xT, wT, vT, y, wt, xm, offs, out):
         g_scales = sb("g_scales", [P, HALF + N], U8)
         nc.vector.memset(g_codes[:, 0:HALF], 0)
         nc.vector.memset(g_scales[:, 0:HALF].bitcast(U32), 0)
-        zeros = shared.tile([P, Q], F32, name="zeros", align_bytes=64, offset=2 * T * 4)
+        zeros = shared.tile([P, Q], F32, name="zeros", align_bytes=256, offset=2 * T * 4)
         nc.vector.memset(zeros[:], 0.0)
 
         x_bf = sb("x_bf", [P, R * PACK], BF16)
@@ -140,9 +140,9 @@ def tile_attend_ghv_lch_kernel(tc, xT, wT, vT, y, wt, xm, offs, out):
         z = sb("z", [P, N, PACK], F32)
         q = sb("q", [P, N, PACK], F32)
         q2 = [sb(f"q2_{n}", [P, Q, PACK], F32) for n in range(QUARTERS - 1)]
-        q2.append(shared.tile([P, Q, PACK], F32, name="q2_3", align_bytes=64, offset=2 * T * 4 + Q * 4))
+        q2.append(shared.tile([P, Q, PACK], F32, name="q2_3", align_bytes=256, offset=2 * T * 4 + Q * 4))
         h = [sb(f"h{n}", [P, Q, PACK], F32) for n in range(2)]
-        h.append(shared.tile([P, Q, PACK], F32, name="h2", align_bytes=64, offset=0))
+        h.append(shared.tile([P, Q, PACK], F32, name="h2", align_bytes=256, offset=0))
         h.append(sb("h3", [P, Q, PACK], F32))
 
         def square(n):
@@ -199,7 +199,7 @@ def tile_attend_ghv_lch_kernel(tc, xT, wT, vT, y, wt, xm, offs, out):
             gather_v(t)
         form_h(2)
         form_h(3)
-        warm_codes = shared.tile([P, WARM_ROWS], U32, name="warm_codes", align_bytes=64, offset=2 * T * 4 + Q * 4)
+        warm_codes = shared.tile([P, WARM_ROWS], U32, name="warm_codes", align_bytes=256, offset=2 * T * 4 + Q * 4)
         nc.vector.tensor_copy(out=warm_codes[:].bitcast(I32), in_=x_codes[:, 0:WARM_ROWS].bitcast(I32))
         for n in range(3):
             warm_up(f"bank{n}", warm_codes[:])
@@ -209,13 +209,13 @@ def tile_attend_ghv_lch_kernel(tc, xT, wT, vT, y, wt, xm, offs, out):
         prepare(v_codes, v_scales, v_bf, v_got)
 
         xm_codes = [sb(f"xm_codes{m}", [P, P], U32) for m in range(2)]
-        xm_codes.append(shared.tile([P, P], U32, name="xm_codes2", align_bytes=64, offset=2 * T * 4 - P * 2))
-        xm_codes.append(shared.tile([P, P], U32, name="xm_codes3", align_bytes=64, offset=2 * T * 4 + P * 2))
+        xm_codes.append(shared.tile([P, P], U32, name="xm_codes2", align_bytes=256, offset=2 * T * 4 - P * 2))
+        xm_codes.append(shared.tile([P, P], U32, name="xm_codes3", align_bytes=256, offset=2 * T * 4 + P * 2))
         xm_scales = sb("xm_scales", [P, D], U8)
 
         def round_xm(on_vector, tile_name, m):
             if m == BLOCKS - 1:
-                bf = shared.tile([P, P, PACK], BF16, name=tile_name, align_bytes=64, offset=3 * T * 4)
+                bf = shared.tile([P, P, PACK], BF16, name=tile_name, align_bytes=256, offset=3 * T * 4)
             else:
                 bf = sb(tile_name, [P, P, PACK], BF16)
             interleave(on_vector, bf[:], xm_block[m])
@@ -267,7 +267,7 @@ def tile_attend_ghv_lch_kernel(tc, xT, wT, vT, y, wt, xm, offs, out):
             )
             return dw
 
-        dense = [shared.tile([P, N], F32, name="dense0", align_bytes=64, offset=3 * T * 4)]
+        dense = [shared.tile([P, N], F32, name="dense0", align_bytes=256, offset=3 * T * 4)]
         dense.extend(sb(f"dense{m}", [P, N], F32) for m in range(1, BLOCKS))
 
         for n in range(QUARTERS - 1):

@@ -24,6 +24,8 @@ HALF = N // 2
 PER_COLUMN = 16
 BLOCKS = D // P
 WARM_ROWS = 32
+ALIGN = 256
+KIB = 1024
 
 
 def tile_attend_ghv_lch_kernel(tc, xT, wT, vT, y, wt, xm, offs, out):
@@ -34,38 +36,45 @@ def tile_attend_ghv_lch_kernel(tc, xT, wT, vT, y, wt, xm, offs, out):
         psum = ctx.enter_context(tc.psum_pool(name="psum", bufs=1))
 
         def sb(name, shape, dtype):
-            return keep.tile(shape, dtype, name=name, align_bytes=256)
+            return keep.tile(shape, dtype, name=name, align_bytes=ALIGN)
+
+        def placed(name, shape, dtype, offset):
+            return shared.tile(shape, dtype, name=name, align_bytes=ALIGN, offset=offset)
+
+        AT_V2, AT_Q2, AT_ZEROS, AT_DENSE, AT_WBF, AT_VBF = 0, 8 * KIB, 11 * KIB, 12 * KIB, 14 * KIB, 15 * KIB
 
         quarter = [slice(n * Q, (n + 1) * Q) for n in range(QUARTERS)]
         half = [slice(0, HALF), slice(HALF, N)]
         block = [slice(m * P, (m + 1) * P) for m in range(BLOCKS)]
 
-        offsets = keep.tile([P, N // PER_COLUMN], U16, name="offsets")
-        half_offsets = [offsets[:, 0 : HALF // PER_COLUMN], offsets[:, HALF // PER_COLUMN : N // PER_COLUMN]]
+        offsets = keep.tile([P, N // PER_COLUMN], U16, name="offsets", align_bytes=ALIGN)
+
+        def listed(slots):
+            return offsets[:, slots.start // PER_COLUMN : slots.stop // PER_COLUMN]
+
         x_raw = sb("x_raw", [P, PACK, R], F32)
-        w_early = sb("w_early", [P, PACK - 1, T], F32)
-        w_last = sb("w_last", [P, T], F32)
-        v_pair = shared.tile([P, 2, T], F32, name="v_pair", align_bytes=256, offset=0)
-        v_late = [sb(f"v_late{u}", [P, T], F32) for u in range(2)]
-        w_plane = [w_early[:, t, :] for t in range(PACK - 1)] + [w_last[:]]
-        v_plane = [v_pair[:, 0, :], v_pair[:, 1, :], v_late[0][:], v_late[1][:]]
+        w_pair = sb("w_pair", [P, 2, T], F32)
+        w_late = [sb(f"w_late{u}", [P, T], F32) for u in range(2)]
+        v_pair = sb("v_pair", [P, 2, T], F32)
+        v_late = [placed("v_late0", [P, T], F32, AT_V2), sb("v_late1", [P, T], F32)]
         y_sb = sb("y_sb", [P, PACK, N], F32)
         wt_sb = sb("wt_sb", [P, PACK], F32)
         xm_first = sb("xm_first", [P, PACK, P], F32)
         xm_rest = sb("xm_rest", [P, PACK, D - P], F32)
         xm_block = [xm_first[:]] + [xm_rest[:, :, block[m]] for m in range(BLOCKS - 1)]
 
-        w_rows = wT.rearrange("(p t) c -> p t c", t=PACK)
-        v_rows = vT.rearrange("(p t) c -> p t c", t=PACK)
+        def load_table(table, pair, late):
+            rows = table.rearrange("(p t) c -> p t c", t=PACK)
+            nc.sync.dma_start(out=pair[:], in_=rows[:, 0:2, :])
+            for u in range(2):
+                nc.sync.dma_start(out=late[u][:], in_=rows[:, 2 + u, :])
+
         nc.scalar.dma_start(out=wt_sb[:], in_=wt.rearrange("b (p t) o -> p (b t o)", t=PACK))
         nc.sync.dma_start(out=x_raw[:], in_=xT.rearrange("b (p t) r -> p (b t) r", t=PACK))
         nc.sync.dma_start(offsets[:], offs)
-        nc.sync.dma_start(out=w_early[:], in_=w_rows[:, 0 : PACK - 1, :])
-        nc.sync.dma_start(out=w_last[:], in_=w_rows[:, PACK - 1, :])
+        load_table(wT, w_pair, w_late)
         nc.sync.dma_start(out=y_sb[:], in_=y.rearrange("b (p t) i -> p (b t) i", t=PACK))
-        nc.sync.dma_start(out=v_pair[:], in_=v_rows[:, 0:2, :])
-        for u in range(2):
-            nc.sync.dma_start(out=v_late[u][:], in_=v_rows[:, 2 + u, :])
+        load_table(vT, v_pair, v_late)
         xm_rows = xm.rearrange("b (p t) d -> p (b t) d", t=PACK)
         nc.sync.dma_start(out=xm_first[:], in_=xm_rows[:, :, 0:P])
         nc.sync.dma_start(out=xm_rest[:], in_=xm_rows[:, :, P:D])
@@ -73,11 +82,7 @@ def tile_attend_ghv_lch_kernel(tc, xT, wT, vT, y, wt, xm, offs, out):
         wide = [sb(f"wide{m}", [P, T], F32) for m in range(BLOCKS)]
         for m in range(BLOCKS):
             nc.vector.memset(wide[m][:].bitcast(U32), 0)
-        g_codes = sb("g_codes", [P, HALF + N], U32)
-        g_scales = sb("g_scales", [P, HALF + N], U8)
-        nc.vector.memset(g_codes[:, 0:HALF], 0)
-        nc.vector.memset(g_scales[:, 0:HALF].bitcast(U32), 0)
-        zeros = shared.tile([P, Q], F32, name="zeros", align_bytes=256, offset=2 * T * 4)
+        zeros = placed("zeros", [P, Q], F32, AT_ZEROS)
         nc.vector.memset(zeros[:], 0.0)
 
         x_bf = sb("x_bf", [P, R * PACK], BF16)
@@ -89,61 +94,74 @@ def tile_attend_ghv_lch_kernel(tc, xT, wT, vT, y, wt, xm, offs, out):
         )
         nc.vector.quantize_mx(out=x_codes[:].bitcast(E4M3), scales=x_scales[:], in_=x_bf[:])
 
+        def in_half(halves, slots):
+            u = slots.start // HALF
+            return halves[u][:, slots.start - u * HALF : slots.stop - u * HALF]
+
         def scores(bank_name, codes, scales, n):
             bank = psum.tile([P, PACK, Q], F32, name=bank_name)
             for t in range(PACK):
-                x_cols = slice(t * P, (t + 1) * P)
                 nc.tensor.matmul_mx(
                     out=bank[:, t, :],
-                    lhsT=x_codes[:, x_cols].bitcast(E4M3),
-                    lhsT_scale=x_scales[:, x_cols],
-                    rhs=codes[:, quarter[n]].bitcast(E4M3),
+                    lhsT=x_codes[:, block[t]].bitcast(E4M3),
+                    lhsT_scale=x_scales[:, block[t]],
+                    rhs=in_half(codes, quarter[n]).bitcast(E4M3),
                     rhs_scale=scales[:, quarter[n]],
                     start=True,
                     stop=True,
                 )
             return bank
 
-        def interleave(on_vector, dst, src):
-            copy = nc.vector.tensor_copy if on_vector else nc.scalar.copy
-            copy(
-                out=dst.rearrange("p (c i) t -> p c t i", i=4),
-                in_=src.rearrange("p t (c i) -> p c t i", i=4),
-            )
+        def gather_early(got, pair, t):
+            nc.scalar.activation(out=got[0][:, t, :], in_=pair[:, t, :].indirect(listed(half[0])), func=ACT.Copy)
+            nc.vector.tensor_copy(got[1][:, t, :], pair[:, t, :].indirect(listed(half[1])))
 
-        def quantize(codes, scales, src, cols):
-            nc.vector.quantize_mx(
-                out=codes[:, cols].bitcast(E4M3),
-                scales=scales[:, cols],
-                in_=src[:, cols, :].rearrange("p c t -> p (c t)"),
-            )
+        pieces = [quarter[0], quarter[1], half[1]]
 
-        def prepare(codes, scales, bf, got):
-            interleave(True, bf[:, quarter[0], :], got[:, :, quarter[0]])
-            interleave(False, bf[:, quarter[1], :], got[:, :, quarter[1]])
-            interleave(True, bf[:, quarter[2], :], got[:, :, quarter[2]])
-            quantize(codes, scales, bf, quarter[0])
-            interleave(True, bf[:, quarter[3], :], got[:, :, quarter[3]])
-            for n in range(1, QUARTERS):
-                quantize(codes, scales, bf, quarter[n])
+        def rounded(name, first_at):
+            bf = [placed(f"{name}0", [P, Q, PACK], BF16, first_at)]
+            bf.append(sb(f"{name}1", [P, Q, PACK], BF16))
+            bf.append(sb(f"{name}2", [P, HALF, PACK], BF16))
+            return bf
 
-        w_got = sb("w_got", [P, PACK, N], F32)
-        w_bf = sb("w_bf", [P, N, PACK], BF16)
-        w_codes = sb("w_codes", [P, N], U32)
-        w_scales = sb("w_scales", [P, N], U8)
-        for t in range(PACK - 1):
-            nc.vector.tensor_copy(w_got[:, t, :], w_plane[t].indirect(offsets[:]))
-        for u in range(2):
-            nc.vector.tensor_copy(w_got[:, PACK - 1, half[u]], w_plane[PACK - 1].indirect(half_offsets[u]))
-        prepare(w_codes, w_scales, w_bf, w_got)
+        def coded(name, last_at):
+            first = sb(f"{name}_codes", [P, HALF], U32)
+            last = placed(f"{name}_codes_last", [P, HALF], U32, last_at)
+            return [first, last], sb(f"{name}_scales", [P, N], U8)
+
+        def place_early(bf, got):
+            for n in range(2):
+                nc.scalar.copy(out=bf[n][:, :, 0:2], in_=got[0][:, :, quarter[n]].rearrange("p t c -> p c t"))
+            nc.vector.tensor_copy(out=bf[2][:, :, 0:2], in_=got[1][:].rearrange("p t c -> p c t"))
+
+        def gather_late(bf, plane, t):
+            for n in range(2):
+                nc.scalar.activation(out=bf[n][:, :, t], in_=plane[:].indirect(listed(pieces[n])), func=ACT.Copy)
+            nc.vector.tensor_copy(bf[2][:, :, t], plane[:].indirect(listed(pieces[2])))
+
+        def quantize(codes, scales, bf):
+            for n, slots in enumerate(pieces):
+                nc.vector.quantize_mx(
+                    out=in_half(codes, slots).bitcast(E4M3),
+                    scales=scales[:, slots],
+                    in_=bf[n][:].rearrange("p c t -> p (c t)"),
+                )
+
+        w_got = [sb(f"w_got{u}", [P, 2, HALF], F32) for u in range(2)]
+        w_bf = rounded("w_bf", AT_WBF)
+        w_codes, w_scales = coded("w", AT_WBF)
+        for t in range(2):
+            gather_early(w_got, w_pair, t)
+        place_early(w_bf, w_got)
+        gather_late(w_bf, w_late[0], 2)
+        gather_late(w_bf, w_late[1], 3)
+        quantize(w_codes, w_scales, w_bf)
 
         z = sb("z", [P, N, PACK], F32)
         q = sb("q", [P, N, PACK], F32)
         q2 = [sb(f"q2_{n}", [P, Q, PACK], F32) for n in range(QUARTERS - 1)]
-        q2.append(shared.tile([P, Q, PACK], F32, name="q2_3", align_bytes=256, offset=2 * T * 4 + Q * 4))
-        h = [sb(f"h{n}", [P, Q, PACK], F32) for n in range(2)]
-        h.append(shared.tile([P, Q, PACK], F32, name="h2", align_bytes=256, offset=0))
-        h.append(sb("h3", [P, Q, PACK], F32))
+        q2.append(placed("q2_3", [P, Q, PACK], F32, AT_Q2))
+        h = sb("h", [P, N, PACK], F32)
 
         def square(n):
             nc.scalar.activation(out=q2[n][:], in_=q[:, quarter[n], :], func=ACT.Square)
@@ -166,7 +184,7 @@ def tile_attend_ghv_lch_kernel(tc, xT, wT, vT, y, wt, xm, offs, out):
 
         def form_h(n):
             nc.vector.scalar_tensor_tensor(
-                out=h[n][:],
+                out=h[:, quarter[n], :],
                 in0=q2[n][:],
                 scalar=1.0,
                 in1=neg_wt[:].unsqueeze(1).to_broadcast([P, Q, PACK]),
@@ -174,134 +192,129 @@ def tile_attend_ghv_lch_kernel(tc, xT, wT, vT, y, wt, xm, offs, out):
                 op1=ALU.mult,
             )
 
-        v_bf = sb("v_bf", [P, N, PACK], BF16)
-        v_codes = sb("v_codes", [P, N], U32)
-        v_scales = sb("v_scales", [P, N], U8)
-        v_got = sb("v_got", [P, PACK, N], F32)
+        def warm_up(name, offset, banks):
+            codes = placed(name, [P, WARM_ROWS], U32, offset)
+            nc.vector.tensor_copy(out=codes[:].bitcast(I32), in_=w_codes[0][:, 0:WARM_ROWS].bitcast(I32))
+            for n in banks:
+                bank = psum.tile([P, N], F32, name=f"bank{n}")
+                nc.tensor.matmul_mx(
+                    out=bank[0:WARM_ROWS, :],
+                    lhsT=codes[:].bitcast(E4M3),
+                    lhsT_scale=w_scales[:, 0:WARM_ROWS],
+                    rhs=x_codes[:].bitcast(E4M3),
+                    rhs_scale=x_scales[:],
+                    start=True,
+                    stop=True,
+                )
 
-        def gather_v(t):
-            nc.vector.tensor_copy(v_got[:, t, :], v_plane[t].indirect(offsets[:]))
-
-        def warm_up(bank_name, codes):
-            bank = psum.tile([P, N], F32, name=bank_name)
-            nc.tensor.matmul_mx(
-                out=bank[0:WARM_ROWS, :],
-                lhsT=codes.bitcast(E4M3),
-                lhsT_scale=x_scales[:, 0:WARM_ROWS],
-                rhs=w_codes[:].bitcast(E4M3),
-                rhs_scale=w_scales[:],
-                start=True,
-                stop=True,
-            )
-
-        for t in range(2):
-            form_h(t)
-            gather_v(t)
+        v_got = [sb(f"v_got{u}", [P, 2, HALF], F32) for u in range(2)]
+        v_bf = rounded("v_bf", AT_VBF)
+        v_codes, v_scales = coded("v", AT_VBF)
+        form_h(0)
+        form_h(1)
+        gather_early(v_got, v_pair, 0)
         form_h(2)
+        gather_early(v_got, v_pair, 1)
         form_h(3)
-        warm_codes = shared.tile([P, WARM_ROWS], U32, name="warm_codes", align_bytes=256, offset=2 * T * 4 + Q * 4)
-        nc.vector.tensor_copy(out=warm_codes[:].bitcast(I32), in_=x_codes[:, 0:WARM_ROWS].bitcast(I32))
-        for n in range(3):
-            warm_up(f"bank{n}", warm_codes[:])
-        gather_v(2)
-        for u in range(2):
-            nc.vector.tensor_copy(v_got[:, PACK - 1, half[u]], v_plane[PACK - 1].indirect(half_offsets[u]))
-        prepare(v_codes, v_scales, v_bf, v_got)
+        warm_up("warm_first", AT_Q2, (0, 1))
+        place_early(v_bf, v_got)
+        gather_late(v_bf, v_late[0], 2)
+        warm_up("warm_second", AT_V2, (2, 3))
+        gather_late(v_bf, v_late[1], 3)
+        quantize(v_codes, v_scales, v_bf)
 
         xm_codes = [sb(f"xm_codes{m}", [P, P], U32) for m in range(2)]
-        xm_codes.append(shared.tile([P, P], U32, name="xm_codes2", align_bytes=256, offset=2 * T * 4 - P * 2))
-        xm_codes.append(shared.tile([P, P], U32, name="xm_codes3", align_bytes=256, offset=2 * T * 4 + P * 2))
+        xm_codes.append(placed("xm_codes2", [P, P], U32, AT_ZEROS - P * 2))
+        xm_codes.append(placed("xm_codes3", [P, P], U32, AT_ZEROS + P * 2))
         xm_scales = sb("xm_scales", [P, D], U8)
+        xm_bf = [sb(f"xm_bf{m}", [P, P, PACK], BF16) for m in range(BLOCKS - 1)]
+        xm_bf.append(placed("xm_bf3", [P, P, PACK], BF16, AT_DENSE))
 
-        def round_xm(on_vector, tile_name, m):
-            if m == BLOCKS - 1:
-                bf = shared.tile([P, P, PACK], BF16, name=tile_name, align_bytes=256, offset=3 * T * 4)
-            else:
-                bf = sb(tile_name, [P, P, PACK], BF16)
-            interleave(on_vector, bf[:], xm_block[m])
-            return bf
+        def round_xm(m):
+            nc.scalar.copy(
+                out=xm_bf[m][:].rearrange("p (c i) t -> p c t i", i=4),
+                in_=xm_block[m].rearrange("p t (c i) -> p c t i", i=4),
+            )
 
-        def quantize_xm(bf, m):
+        def quantize_xm(m):
             nc.vector.quantize_mx(
                 out=xm_codes[m][:].bitcast(E4M3),
                 scales=xm_scales[:, block[m]],
-                in_=bf[:].rearrange("p c t -> p (c t)"),
+                in_=xm_bf[m][:].rearrange("p c t -> p (c t)"),
             )
 
-        xm_bf0 = round_xm(False, "xm_bf0", 0)
-        xm_bf1 = round_xm(False, "xm_bf1", 1)
-        xm_bf2 = round_xm(False, "xm_bf2", 2)
-        quantize_xm(xm_bf0, 0)
+        for m in range(BLOCKS - 1):
+            round_xm(m)
+        quantize_xm(0)
 
-        g_bf = sb("g_bf", [P, N - Q, PACK], BF16)
-        g_last = sb("g_last", [P, Q, PACK], BF16)
+        g_bf = sb("g_bf", [P, N, PACK], BF16)
+        g_codes = sb("g_codes", [P, N], U32)
+        g_scales = sb("g_scales", [P, N], U8)
+        av = [scores(f"bank{QUARTERS + n}", v_codes, v_scales, n) for n in range(QUARTERS)]
 
-        def form_g(n, dst, pieces=1):
-            av = scores(f"bank{QUARTERS + n}", v_codes, v_scales, n)
-            for u in range(pieces):
-                cols = slice(u * Q // pieces, (u + 1) * Q // pieces)
-                nc.vector.tensor_tensor(
-                    out=dst[:, cols, :],
-                    in0=av[:, :, cols].rearrange("p t i -> p i t"),
-                    in1=h[n][:, cols, :],
-                    op=ALU.mult,
-                )
+        def form_g(slots):
+            n = slots.start // Q
+            nc.vector.tensor_tensor(
+                out=g_bf[:, slots, :],
+                in0=av[n][:, :, slots.start - n * Q : slots.stop - n * Q].rearrange("p t i -> p i t"),
+                in1=h[:, slots, :],
+                op=ALU.mult,
+            )
 
-        def quantize_g(first, last, src):
+        def quantize_g(slots):
             nc.vector.quantize_mx(
-                out=g_codes[:, HALF + first : HALF + last].bitcast(E5M2),
-                scales=g_scales[:, HALF + first : HALF + last],
-                in_=src.rearrange("p i t -> p (i t)"),
+                out=g_codes[:, slots].bitcast(E5M2),
+                scales=g_scales[:, slots],
+                in_=g_bf[:, slots, :].rearrange("p i t -> p (i t)"),
             )
 
-        def product(bank_name, m, first_col):
-            dw = psum.tile([P, N], F32, name=bank_name)
+        dense = [placed("dense0", [P, N], F32, AT_DENSE)]
+        dense.extend(sb(f"dense{m}", [P, N], F32) for m in range(1, BLOCKS))
+
+        def product(bank_name, m, slots):
+            dw = psum.tile([P, slots.stop - slots.start], F32, name=bank_name)
             nc.tensor.matmul_mx(
                 out=dw[:],
                 lhsT=xm_codes[m][:].bitcast(E4M3),
                 lhsT_scale=xm_scales[:, block[m]],
-                rhs=g_codes[:, first_col : first_col + N].bitcast(E5M2),
-                rhs_scale=g_scales[:, first_col : first_col + N],
+                rhs=g_codes[:, slots].bitcast(E5M2),
+                rhs_scale=g_scales[:, slots],
                 start=True,
                 stop=True,
             )
-            return dw
+            nc.scalar.copy(out=dense[m][:, slots], in_=dw[:])
 
-        dense = [shared.tile([P, N], F32, name="dense0", align_bytes=256, offset=3 * T * 4)]
-        dense.extend(sb(f"dense{m}", [P, N], F32) for m in range(1, BLOCKS))
-
+        eighths = [slice(N - Q, N - Q // 2), slice(N - Q // 2, N)]
         for n in range(QUARTERS - 1):
-            form_g(n, g_bf[:, quarter[n], :])
-        quantize_g(0, HALF, g_bf[:, half[0], :])
-        early = product("bank3", 0, 0)
-        nc.scalar.copy(out=dense[0][:, half[0]], in_=early[:, half[1]])
-        quantize_g(HALF, N - Q, g_bf[:, quarter[2], :])
-        first = product("bank0", 0, Q)
-        nc.scalar.copy(out=dense[0][:, quarter[2]], in_=first[:, quarter[3]])
-        form_g(QUARTERS - 1, g_last[:], 2)
-        quantize_g(N - Q, N - Q // 2, g_last[:, 0 : Q // 2, :])
-        quantize_g(N - Q // 2, N, g_last[:, Q // 2 : Q, :])
-        quantize_xm(xm_bf1, 1)
-        second = product("bank1", 0, HALF)
-        split = (N - Q) // PER_COLUMN
-        nc.vector.tensor_copy(wide[0][:].indirect(offsets[:, 0:split]), dense[0][:, 0 : N - Q])
-        nc.scalar.copy(out=dense[0][:, quarter[3]], in_=second[:, quarter[3]])
+            form_g(quarter[n])
+        quantize_g(half[0])
+        product("bank0", 0, half[0])
+        quantize_g(quarter[2])
+        product("bank1", 0, quarter[2])
+        for slots in eighths:
+            form_g(slots)
+        quantize_g(eighths[0])
+        quantize_xm(1)
+        quantize_g(eighths[1])
+        product("bank2", 0, quarter[3])
+        early = slice(0, N - Q)
+        nc.vector.tensor_copy(wide[0][:].indirect(listed(early)), dense[0][:, early])
         nc.vector.tensor_tensor(
-            out=wide[0][:].indirect(offsets[:, split : N // PER_COLUMN]),
+            out=wide[0][:].indirect(listed(quarter[3])),
             in0=dense[0][:, quarter[3]],
             in1=zeros[:],
             op=ALU.add,
         )
         nc.sync.dma_start(out=out[block[0], :], in_=wide[0][:])
-        quantize_xm(xm_bf2, 2)
-        xm_bf3 = round_xm(False, "xm_bf3", 3)
-        quantize_xm(xm_bf3, 3)
 
         def finish(m):
-            dw = product(f"bank{(m + 1) % QUARTERS}", m, HALF)
-            nc.scalar.copy(out=dense[m][:], in_=dw[:])
+            product(f"bank{(m + 2) % QUARTERS}", m, slice(0, N))
             nc.vector.tensor_copy(wide[m][:].indirect(offsets[:]), dense[m][:])
             nc.sync.dma_start(out=out[block[m], :], in_=wide[m][:])
 
-        for m in range(1, BLOCKS):
-            finish(m)
+        quantize_xm(2)
+        finish(1)
+        round_xm(3)
+        quantize_xm(3)
+        finish(2)
+        finish(3)

@@ -8,7 +8,6 @@ FLOPS = 3 * 2 * D * R * N
 F32 = mybir.dt.float32
 BF16 = mybir.dt.bfloat16
 U32 = mybir.dt.uint32
-I32 = mybir.dt.int32
 U16 = mybir.dt.uint16
 U8 = mybir.dt.uint8
 E4M3 = mybir.dt.float8_e4m3fn_x4
@@ -41,7 +40,8 @@ def tile_attend_ghv_lch_kernel(tc, xT, wT, vT, y, wt, xm, offs, out):
         def placed(name, shape, dtype, offset):
             return shared.tile(shape, dtype, name=name, align_bytes=ALIGN, offset=offset)
 
-        AT_V2, AT_Q2, AT_ZEROS, AT_DENSE, AT_WBF, AT_VBF = 0, 8 * KIB, 11 * KIB, 12 * KIB, 14 * KIB, 15 * KIB
+        AT_V2, AT_H, AT_ZEROS, AT_DENSE, AT_WBF, AT_VBF = 0, 8 * KIB, 11 * KIB, 12 * KIB, 14 * KIB, 16 * KIB
+        AT_VGOT = 18 * KIB
 
         quarter = [slice(n * Q, (n + 1) * Q) for n in range(QUARTERS)]
         half = [slice(0, HALF), slice(HALF, N)]
@@ -94,10 +94,6 @@ def tile_attend_ghv_lch_kernel(tc, xT, wT, vT, y, wt, xm, offs, out):
         )
         nc.vector.quantize_mx(out=x_codes[:].bitcast(E4M3), scales=x_scales[:], in_=x_bf[:])
 
-        def in_half(halves, slots):
-            u = slots.start // HALF
-            return halves[u][:, slots.start - u * HALF : slots.stop - u * HALF]
-
         def scores(bank_name, codes, scales, n):
             bank = psum.tile([P, PACK, Q], F32, name=bank_name)
             for t in range(PACK):
@@ -105,63 +101,69 @@ def tile_attend_ghv_lch_kernel(tc, xT, wT, vT, y, wt, xm, offs, out):
                     out=bank[:, t, :],
                     lhsT=x_codes[:, block[t]].bitcast(E4M3),
                     lhsT_scale=x_scales[:, block[t]],
-                    rhs=in_half(codes, quarter[n]).bitcast(E4M3),
+                    rhs=codes[n][:].bitcast(E4M3),
                     rhs_scale=scales[:, quarter[n]],
                     start=True,
                     stop=True,
                 )
             return bank
 
-        def gather_early(got, pair, t):
-            nc.scalar.activation(out=got[0][:, t, :], in_=pair[:, t, :].indirect(listed(half[0])), func=ACT.Copy)
-            nc.vector.tensor_copy(got[1][:, t, :], pair[:, t, :].indirect(listed(half[1])))
+        def gather(dst, plane, slots):
+            src = plane.indirect(listed(slots))
+            if slots.start < HALF:
+                nc.vector.tensor_copy(dst, src)
+            else:
+                nc.scalar.activation(out=dst, in_=src, func=ACT.Copy)
 
-        pieces = [quarter[0], quarter[1], half[1]]
+        def place(dst, src, n):
+            copy = nc.vector.tensor_copy if n < 2 else nc.scalar.copy
+            copy(out=dst, in_=src)
 
-        def rounded(name, first_at):
-            bf = [placed(f"{name}0", [P, Q, PACK], BF16, first_at)]
-            bf.append(sb(f"{name}1", [P, Q, PACK], BF16))
-            bf.append(sb(f"{name}2", [P, HALF, PACK], BF16))
-            return bf
+        def rounded(name, at):
+            bf = [placed(f"{name}{n}", [P, Q, PACK], BF16, at + n * KIB) for n in range(2)]
+            return bf + [sb(f"{name}{n}", [P, Q, PACK], BF16) for n in range(2, QUARTERS)]
 
-        def coded(name, last_at):
-            first = sb(f"{name}_codes", [P, HALF], U32)
-            last = placed(f"{name}_codes_last", [P, HALF], U32, last_at)
-            return [first, last], sb(f"{name}_scales", [P, N], U8)
+        def coded(name, at):
+            codes = [sb(f"{name}_codes{n}", [P, Q], U32) for n in range(2)]
+            codes.extend(placed(f"{name}_codes{n + 2}", [P, Q], U32, at + n * KIB) for n in range(2))
+            return codes, sb(f"{name}_scales", [P, N], U8)
+
+        def gather_early(got, plane, t):
+            for u in range(2):
+                gather(got[u][:, t, :], plane, half[u])
 
         def place_early(bf, got):
-            for n in range(2):
-                nc.scalar.copy(out=bf[n][:, :, 0:2], in_=got[0][:, :, quarter[n]].rearrange("p t c -> p c t"))
-            nc.vector.tensor_copy(out=bf[2][:, :, 0:2], in_=got[1][:].rearrange("p t c -> p c t"))
+            for n in range(QUARTERS):
+                src = got[n // 2][:, :, quarter[n % 2]].rearrange("p t c -> p c t")
+                place(bf[n][:, :, 0 : PACK - 1], src, n)
 
-        def gather_late(bf, plane, t):
-            for n in range(2):
-                nc.scalar.activation(out=bf[n][:, :, t], in_=plane[:].indirect(listed(pieces[n])), func=ACT.Copy)
-            nc.vector.tensor_copy(bf[2][:, :, t], plane[:].indirect(listed(pieces[2])))
-
-        def quantize(codes, scales, bf):
-            for n, slots in enumerate(pieces):
+        def finish_table(name, codes, scales, bf, plane):
+            last = [sb(f"{name}_last{n}", [P, Q], F32) for n in range(QUARTERS)]
+            for n in range(QUARTERS):
+                gather(last[n][:], plane, quarter[n])
+            for n in range(QUARTERS):
+                place(bf[n][:, :, PACK - 1], last[n][:], n)
+            for n in range(QUARTERS):
                 nc.vector.quantize_mx(
-                    out=in_half(codes, slots).bitcast(E4M3),
-                    scales=scales[:, slots],
+                    out=codes[n][:].bitcast(E4M3),
+                    scales=scales[:, quarter[n]],
                     in_=bf[n][:].rearrange("p c t -> p (c t)"),
                 )
 
-        w_got = [sb(f"w_got{u}", [P, 2, HALF], F32) for u in range(2)]
+        w_got = [sb(f"w_got{u}", [P, PACK - 1, HALF], F32) for u in range(2)]
         w_bf = rounded("w_bf", AT_WBF)
         w_codes, w_scales = coded("w", AT_WBF)
         for t in range(2):
-            gather_early(w_got, w_pair, t)
+            gather_early(w_got, w_pair[:, t, :], t)
+        gather_early(w_got, w_late[0][:], 2)
         place_early(w_bf, w_got)
-        gather_late(w_bf, w_late[0], 2)
-        gather_late(w_bf, w_late[1], 3)
-        quantize(w_codes, w_scales, w_bf)
+        finish_table("w", w_codes, w_scales, w_bf, w_late[1][:])
 
         z = sb("z", [P, N, PACK], F32)
         q = sb("q", [P, N, PACK], F32)
-        q2 = [sb(f"q2_{n}", [P, Q, PACK], F32) for n in range(QUARTERS - 1)]
-        q2.append(placed("q2_3", [P, Q, PACK], F32, AT_Q2))
-        h = sb("h", [P, N, PACK], F32)
+        q2 = [sb(f"q2_{n}", [P, Q, PACK], F32) for n in range(QUARTERS)]
+        h = [placed("h0", [P, Q, PACK], F32, AT_H)]
+        h.extend(sb(f"h{n}", [P, Q, PACK], F32) for n in range(1, QUARTERS))
 
         def square(n):
             nc.scalar.activation(out=q2[n][:], in_=q[:, quarter[n], :], func=ACT.Square)
@@ -184,7 +186,7 @@ def tile_attend_ghv_lch_kernel(tc, xT, wT, vT, y, wt, xm, offs, out):
 
         def form_h(n):
             nc.vector.scalar_tensor_tensor(
-                out=h[:, quarter[n], :],
+                out=h[n][:],
                 in0=q2[n][:],
                 scalar=1.0,
                 in1=neg_wt[:].unsqueeze(1).to_broadcast([P, Q, PACK]),
@@ -194,7 +196,7 @@ def tile_attend_ghv_lch_kernel(tc, xT, wT, vT, y, wt, xm, offs, out):
 
         def warm_up(name, offset, banks):
             codes = placed(name, [P, WARM_ROWS], U32, offset)
-            nc.vector.tensor_copy(out=codes[:].bitcast(I32), in_=w_codes[0][:, 0:WARM_ROWS].bitcast(I32))
+            nc.scalar.copy(out=codes[:], in_=w_codes[0][:, 0:WARM_ROWS])
             for n in banks:
                 bank = psum.tile([P, N], F32, name=f"bank{n}")
                 nc.tensor.matmul_mx(
@@ -207,23 +209,22 @@ def tile_attend_ghv_lch_kernel(tc, xT, wT, vT, y, wt, xm, offs, out):
                     stop=True,
                 )
 
-        v_got = [sb(f"v_got{u}", [P, 2, HALF], F32) for u in range(2)]
+        v_got = [sb("v_got0", [P, PACK - 1, HALF], F32), placed("v_got1", [P, PACK - 1, HALF], F32, AT_VGOT)]
         v_bf = rounded("v_bf", AT_VBF)
         v_codes, v_scales = coded("v", AT_VBF)
         form_h(0)
         form_h(1)
-        gather_early(v_got, v_pair, 0)
+        gather_early(v_got, v_pair[:, 0, :], 0)
         form_h(2)
-        gather_early(v_got, v_pair, 1)
+        gather_early(v_got, v_pair[:, 1, :], 1)
         form_h(3)
-        warm_up("warm_first", AT_Q2, (0, 1))
+        gather_early(v_got, v_late[0][:], 2)
+        warm_up("warm_first", AT_V2, (0, 1))
         place_early(v_bf, v_got)
-        gather_late(v_bf, v_late[0], 2)
-        warm_up("warm_second", AT_V2, (2, 3))
-        gather_late(v_bf, v_late[1], 3)
-        quantize(v_codes, v_scales, v_bf)
+        warm_up("warm_second", AT_VGOT, (2, 3))
+        finish_table("v", v_codes, v_scales, v_bf, v_late[1][:])
 
-        xm_codes = [sb(f"xm_codes{m}", [P, P], U32) for m in range(2)]
+        xm_codes = [placed("xm_codes0", [P, P], U32, AT_H), sb("xm_codes1", [P, P], U32)]
         xm_codes.append(placed("xm_codes2", [P, P], U32, AT_ZEROS - P * 2))
         xm_codes.append(placed("xm_codes3", [P, P], U32, AT_ZEROS + P * 2))
         xm_scales = sb("xm_scales", [P, D], U8)
@@ -245,7 +246,6 @@ def tile_attend_ghv_lch_kernel(tc, xT, wT, vT, y, wt, xm, offs, out):
 
         for m in range(BLOCKS - 1):
             round_xm(m)
-        quantize_xm(0)
 
         g_bf = sb("g_bf", [P, N, PACK], BF16)
         g_codes = sb("g_codes", [P, N], U32)
@@ -254,10 +254,11 @@ def tile_attend_ghv_lch_kernel(tc, xT, wT, vT, y, wt, xm, offs, out):
 
         def form_g(slots):
             n = slots.start // Q
+            own = slice(slots.start - n * Q, slots.stop - n * Q)
             nc.vector.tensor_tensor(
                 out=g_bf[:, slots, :],
-                in0=av[n][:, :, slots.start - n * Q : slots.stop - n * Q].rearrange("p t i -> p i t"),
-                in1=h[:, slots, :],
+                in0=av[n][:, :, own].rearrange("p t i -> p i t"),
+                in1=h[n][:, own, :],
                 op=ALU.mult,
             )
 
@@ -285,8 +286,10 @@ def tile_attend_ghv_lch_kernel(tc, xT, wT, vT, y, wt, xm, offs, out):
             nc.scalar.copy(out=dense[m][:, slots], in_=dw[:])
 
         eighths = [slice(N - Q, N - Q // 2), slice(N - Q // 2, N)]
-        for n in range(QUARTERS - 1):
-            form_g(quarter[n])
+        form_g(quarter[0])
+        form_g(quarter[1])
+        quantize_xm(0)
+        form_g(quarter[2])
         quantize_g(half[0])
         product("bank0", 0, half[0])
         quantize_g(quarter[2])

@@ -40,8 +40,7 @@ def tile_attend_ghv_lch_kernel(tc, xT, wT, vT, y, wt, xm, offs, out):
         def placed(name, shape, dtype, offset):
             return shared.tile(shape, dtype, name=name, align_bytes=ALIGN, offset=offset)
 
-        AT_V2, AT_H, AT_ZEROS, AT_DENSE, AT_WBF, AT_VBF = 0, 8 * KIB, 11 * KIB, 12 * KIB, 14 * KIB, 16 * KIB
-        AT_VGOT = 18 * KIB
+        AT_Q2, AT_H, AT_ZEROS, AT_DENSE, AT_WBF, AT_VBF, AT_VGOT = [KIB * k for k in (0, 2, 5, 6, 8, 10, 12)]
 
         quarter = [slice(n * Q, (n + 1) * Q) for n in range(QUARTERS)]
         half = [slice(0, HALF), slice(HALF, N)]
@@ -56,7 +55,7 @@ def tile_attend_ghv_lch_kernel(tc, xT, wT, vT, y, wt, xm, offs, out):
         w_pair = sb("w_pair", [P, 2, T], F32)
         w_late = [sb(f"w_late{u}", [P, T], F32) for u in range(2)]
         v_pair = sb("v_pair", [P, 2, T], F32)
-        v_late = [placed("v_late0", [P, T], F32, AT_V2), sb("v_late1", [P, T], F32)]
+        v_late = [sb(f"v_late{u}", [P, T], F32) for u in range(2)]
         y_sb = sb("y_sb", [P, PACK, N], F32)
         wt_sb = sb("wt_sb", [P, PACK], F32)
         xm_first = sb("xm_first", [P, PACK, P], F32)
@@ -161,12 +160,16 @@ def tile_attend_ghv_lch_kernel(tc, xT, wT, vT, y, wt, xm, offs, out):
 
         z = sb("z", [P, N, PACK], F32)
         q = sb("q", [P, N, PACK], F32)
-        q2 = [sb(f"q2_{n}", [P, Q, PACK], F32) for n in range(QUARTERS)]
+        q2 = [sb(f"q2_{n}", [P, Q, PACK], F32) for n in range(QUARTERS - 1)]
+        q2.append(placed("q2_3", [P, Q, PACK], F32, AT_Q2))
         h = [placed("h0", [P, Q, PACK], F32, AT_H)]
         h.extend(sb(f"h{n}", [P, Q, PACK], F32) for n in range(1, QUARTERS))
 
         def square(n):
-            nc.scalar.activation(out=q2[n][:], in_=q[:, quarter[n], :], func=ACT.Square)
+            if n < 2:
+                nc.vector.tensor_tensor(out=q2[n][:], in0=q[:, quarter[n], :], in1=q[:, quarter[n], :], op=ALU.mult)
+            else:
+                nc.scalar.activation(out=q2[n][:], in_=q[:, quarter[n], :], func=ACT.Square)
 
         for n in range(QUARTERS):
             a = scores(f"bank{n}", w_codes, w_scales, n)
@@ -177,9 +180,8 @@ def tile_attend_ghv_lch_kernel(tc, xT, wT, vT, y, wt, xm, offs, out):
                 op=ALU.subtract,
             )
             nc.scalar.activation(out=q[:, quarter[n], :], in_=z[:, quarter[n], :], func=ACT.Tanh)
-            if n > 0:
-                square(n - 1)
-        square(QUARTERS - 1)
+        for n in range(QUARTERS):
+            square(n)
 
         neg_wt = sb("neg_wt", [P, PACK], F32)
         nc.vector.tensor_scalar(out=neg_wt[:], in0=wt_sb[:], scalar1=-1.0, scalar2=None, op0=ALU.mult)
@@ -218,8 +220,8 @@ def tile_attend_ghv_lch_kernel(tc, xT, wT, vT, y, wt, xm, offs, out):
         form_h(2)
         gather_early(v_got, v_pair[:, 1, :], 1)
         form_h(3)
+        warm_up("warm_first", AT_Q2, (0, 1))
         gather_early(v_got, v_late[0][:], 2)
-        warm_up("warm_first", AT_V2, (0, 1))
         place_early(v_bf, v_got)
         warm_up("warm_second", AT_VGOT, (2, 3))
         finish_table("v", v_codes, v_scales, v_bf, v_late[1][:])

@@ -110,12 +110,12 @@ def tile_attend_ghv_lch_kernel(tc, xT, wT, vT, y, wt, xm, offs, out):
         def gather(dst, plane, slots):
             src = plane.indirect(listed(slots))
             if slots.start < HALF:
-                nc.vector.tensor_copy(dst, src)
-            else:
                 nc.scalar.activation(out=dst, in_=src, func=ACT.Copy)
+            else:
+                nc.vector.tensor_copy(dst, src)
 
         def place(dst, src, n):
-            copy = nc.vector.tensor_copy if n < 2 else nc.scalar.copy
+            copy = nc.scalar.copy if n < 2 else nc.vector.tensor_copy
             copy(out=dst, in_=src)
 
         def rounded(name, at):
@@ -137,17 +137,22 @@ def tile_attend_ghv_lch_kernel(tc, xT, wT, vT, y, wt, xm, offs, out):
                 place(bf[n][:, :, 0 : PACK - 1], src, n)
 
         def finish_table(name, codes, scales, bf, plane):
-            last = [sb(f"{name}_last{n}", [P, Q], F32) for n in range(QUARTERS)]
-            for n in range(QUARTERS):
-                gather(last[n][:], plane, quarter[n])
-            for n in range(QUARTERS):
-                place(bf[n][:, :, PACK - 1], last[n][:], n)
-            for n in range(QUARTERS):
+            def quantize(n):
                 nc.vector.quantize_mx(
                     out=codes[n][:].bitcast(E4M3),
                     scales=scales[:, quarter[n]],
                     in_=bf[n][:].rearrange("p c t -> p (c t)"),
                 )
+
+            last = [sb(f"{name}_last{n}", [P, Q], F32) for n in range(2)]
+            for n in range(2):
+                gather(bf[n][:, :, PACK - 1], plane, quarter[n])
+                gather(last[n][:], plane, quarter[2 + n])
+            quantize(0)
+            for n in range(2):
+                place(bf[2 + n][:, :, PACK - 1], last[n][:], 2 + n)
+            for n in range(1, QUARTERS):
+                quantize(n)
 
         w_got = [sb(f"w_got{u}", [P, PACK - 1, HALF], F32) for u in range(2)]
         w_bf = rounded("w_bf", AT_WBF)
@@ -166,7 +171,7 @@ def tile_attend_ghv_lch_kernel(tc, xT, wT, vT, y, wt, xm, offs, out):
         h.extend(sb(f"h{n}", [P, Q, PACK], F32) for n in range(1, QUARTERS))
 
         def square(n):
-            if n < 2:
+            if n == 0:
                 nc.vector.tensor_tensor(out=q2[n][:], in0=q[:, quarter[n], :], in1=q[:, quarter[n], :], op=ALU.mult)
             else:
                 nc.scalar.activation(out=q2[n][:], in_=q[:, quarter[n], :], func=ACT.Square)
@@ -196,9 +201,9 @@ def tile_attend_ghv_lch_kernel(tc, xT, wT, vT, y, wt, xm, offs, out):
                 op1=ALU.mult,
             )
 
-        def warm_up(name, offset, banks):
+        def warm_up(name, copy, offset, banks):
             codes = placed(name, [P, WARM_ROWS], U32, offset)
-            nc.scalar.copy(out=codes[:], in_=w_codes[0][:, 0:WARM_ROWS])
+            copy(out=codes[:], in_=w_codes[0][:, 0:WARM_ROWS])
             for n in banks:
                 bank = psum.tile([P, N], F32, name=f"bank{n}")
                 nc.tensor.matmul_mx(
@@ -220,10 +225,10 @@ def tile_attend_ghv_lch_kernel(tc, xT, wT, vT, y, wt, xm, offs, out):
         form_h(2)
         gather_early(v_got, v_pair[:, 1, :], 1)
         form_h(3)
-        warm_up("warm_first", AT_Q2, (0, 1))
+        warm_up("warm_first", nc.scalar.copy, AT_Q2, (0, 1))
         gather_early(v_got, v_late[0][:], 2)
         place_early(v_bf, v_got)
-        warm_up("warm_second", AT_VGOT, (2, 3))
+        warm_up("warm_second", nc.vector.tensor_copy, AT_VGOT, (2, 3))
         finish_table("v", v_codes, v_scales, v_bf, v_late[1][:])
 
         xm_codes = [placed("xm_codes0", [P, P], U32, AT_H), sb("xm_codes1", [P, P], U32)]

@@ -40,7 +40,7 @@ def tile_attend_ghv_lch_kernel(tc, xT, wT, vT, y, wt, xm, offs, out):
         def placed(name, shape, dtype, offset):
             return shared.tile(shape, dtype, name=name, align_bytes=ALIGN, offset=offset)
 
-        AT_Q2, AT_H, AT_ZEROS, AT_DENSE, AT_WBF, AT_VBF, AT_VGOT = [KIB * k for k in (0, 2, 5, 6, 8, 10, 12)]
+        AT_Q2, AT_ZEROS, AT_DENSE, AT_WBF, AT_VBF, AT_H, AT_THIRD = [KIB * k for k in (0, 5, 6, 8, 10, 12, 14)]
 
         quarter = [slice(n * Q, (n + 1) * Q) for n in range(QUARTERS)]
         half = [slice(0, HALF), slice(HALF, N)]
@@ -55,7 +55,7 @@ def tile_attend_ghv_lch_kernel(tc, xT, wT, vT, y, wt, xm, offs, out):
         w_pair = sb("w_pair", [P, 2, T], F32)
         w_late = [sb(f"w_late{u}", [P, T], F32) for u in range(2)]
         v_pair = sb("v_pair", [P, 2, T], F32)
-        v_late = [sb(f"v_late{u}", [P, T], F32) for u in range(2)]
+        v_late = [placed("v_late0", [P, T], F32, AT_THIRD), sb("v_late1", [P, T], F32)]
         y_sb = sb("y_sb", [P, PACK, N], F32)
         wt_sb = sb("wt_sb", [P, PACK], F32)
         xm_first = sb("xm_first", [P, PACK, P], F32)
@@ -107,60 +107,63 @@ def tile_attend_ghv_lch_kernel(tc, xT, wT, vT, y, wt, xm, offs, out):
                 )
             return bank
 
-        def gather(dst, plane, slots):
-            src = plane.indirect(listed(slots))
-            if slots.start < HALF:
-                nc.scalar.activation(out=dst, in_=src, func=ACT.Copy)
-            else:
-                nc.vector.tensor_copy(dst, src)
+        def gather_on_vector(dst, plane, slots):
+            nc.vector.tensor_copy(dst, plane.indirect(listed(slots)))
 
-        def place(dst, src, n):
-            copy = nc.scalar.copy if n < 2 else nc.vector.tensor_copy
-            copy(out=dst, in_=src)
+        def gather_on_scalar(dst, plane, slots):
+            nc.scalar.activation(out=dst, in_=plane.indirect(listed(slots)), func=ACT.Copy)
 
         def rounded(name, at):
-            bf = [placed(f"{name}{n}", [P, Q, PACK], BF16, at + n * KIB) for n in range(2)]
-            return bf + [sb(f"{name}{n}", [P, Q, PACK], BF16) for n in range(2, QUARTERS)]
+            bf = [placed(f"{name}0", [P, Q, PACK], BF16, at)]
+            return bf + [sb(f"{name}{n}", [P, Q, PACK], BF16) for n in range(1, QUARTERS)]
 
         def coded(name, at):
-            codes = [sb(f"{name}_codes{n}", [P, Q], U32) for n in range(2)]
-            codes.extend(placed(f"{name}_codes{n + 2}", [P, Q], U32, at + n * KIB) for n in range(2))
-            return codes, sb(f"{name}_scales", [P, N], U8)
+            codes = [sb(f"{name}_codes{n}", [P, Q], U32) for n in (0, 1, 3)]
+            return codes[0:2] + [placed(f"{name}_codes2", [P, Q], U32, at), codes[2]], sb(f"{name}_scales", [P, N], U8)
 
-        def gather_early(got, plane, t):
-            for u in range(2):
-                gather(got[u][:, t, :], plane, half[u])
+        def gather_front(front, plane, t):
+            gather_on_scalar(front[0][:, t, :], plane, half[0])
+            gather_on_vector(front[1][:, t, :], plane, half[1])
 
-        def place_early(bf, got):
-            for n in range(QUARTERS):
-                src = got[n // 2][:, :, quarter[n % 2]].rearrange("p t c -> p c t")
-                place(bf[n][:, :, 0 : PACK - 1], src, n)
+        def place_front(bf, front, n):
+            copy = nc.scalar.copy if n == 0 else nc.vector.tensor_copy
+            copy(out=bf[n][:, :, 0:2], in_=front[n // 2][:, :, quarter[n % 2]].rearrange("p t c -> p c t"))
+
+        def gather_back(bf, staged, plane, t):
+            for n in (0, 1, 3):
+                gather_on_scalar(bf[n][:, :, t], plane, quarter[n])
+            gather_on_vector(staged[:], plane, quarter[2])
+
+        def place_back(bf, staged, t):
+            nc.vector.tensor_copy(out=bf[2][:, :, t], in_=staged[:])
+
+        def quantize_table(codes, scales, bf, n):
+            nc.vector.quantize_mx(
+                out=codes[n][:].bitcast(E4M3),
+                scales=scales[:, quarter[n]],
+                in_=bf[n][:].rearrange("p c t -> p (c t)"),
+            )
 
         def finish_table(name, codes, scales, bf, plane):
-            def quantize(n):
-                nc.vector.quantize_mx(
-                    out=codes[n][:].bitcast(E4M3),
-                    scales=scales[:, quarter[n]],
-                    in_=bf[n][:].rearrange("p c t -> p (c t)"),
-                )
-
             last = [sb(f"{name}_last{n}", [P, Q], F32) for n in range(2)]
             for n in range(2):
-                gather(bf[n][:, :, PACK - 1], plane, quarter[n])
-                gather(last[n][:], plane, quarter[2 + n])
-            quantize(0)
-            for n in range(2):
-                place(bf[2 + n][:, :, PACK - 1], last[n][:], 2 + n)
-            for n in range(1, QUARTERS):
-                quantize(n)
+                gather_on_scalar(bf[n][:, :, 3], plane, quarter[n])
+                gather_on_vector(last[n][:], plane, quarter[2 + n])
+            nc.scalar.copy(out=bf[3][:, :, 3], in_=last[1][:])
+            place_back(bf, last[0], 3)
+            for n in range(QUARTERS):
+                quantize_table(codes, scales, bf, n)
 
-        w_got = [sb(f"w_got{u}", [P, PACK - 1, HALF], F32) for u in range(2)]
+        w_front = [sb(f"w_front{u}", [P, 2, HALF], F32) for u in range(2)]
+        w_third = sb("w_third", [P, Q], F32)
         w_bf = rounded("w_bf", AT_WBF)
         w_codes, w_scales = coded("w", AT_WBF)
         for t in range(2):
-            gather_early(w_got, w_pair[:, t, :], t)
-        gather_early(w_got, w_late[0][:], 2)
-        place_early(w_bf, w_got)
+            gather_front(w_front, w_pair[:, t, :], t)
+        for n in range(QUARTERS):
+            place_front(w_bf, w_front, n)
+        gather_back(w_bf, w_third, w_late[0][:], 2)
+        place_back(w_bf, w_third, 2)
         finish_table("w", w_codes, w_scales, w_bf, w_late[1][:])
 
         z = sb("z", [P, N, PACK], F32)
@@ -216,19 +219,21 @@ def tile_attend_ghv_lch_kernel(tc, xT, wT, vT, y, wt, xm, offs, out):
                     stop=True,
                 )
 
-        v_got = [sb("v_got0", [P, PACK - 1, HALF], F32), placed("v_got1", [P, PACK - 1, HALF], F32, AT_VGOT)]
+        v_front = [sb(f"v_front{u}", [P, 2, HALF], F32) for u in range(2)]
+        v_third = sb("v_third", [P, Q], F32)
         v_bf = rounded("v_bf", AT_VBF)
         v_codes, v_scales = coded("v", AT_VBF)
-        form_h(0)
-        form_h(1)
-        gather_early(v_got, v_pair[:, 0, :], 0)
-        form_h(2)
-        gather_early(v_got, v_pair[:, 1, :], 1)
-        form_h(3)
+        for n in range(QUARTERS):
+            form_h(n)
+        for t in range(2):
+            gather_front(v_front, v_pair[:, t, :], t)
+        place_front(v_bf, v_front, 0)
         warm_up("warm_first", nc.scalar.copy, AT_Q2, (0, 1))
-        gather_early(v_got, v_late[0][:], 2)
-        place_early(v_bf, v_got)
-        warm_up("warm_second", nc.vector.tensor_copy, AT_VGOT, (2, 3))
+        for n in range(1, QUARTERS):
+            place_front(v_bf, v_front, n)
+        gather_back(v_bf, v_third, v_late[0][:], 2)
+        place_back(v_bf, v_third, 2)
+        warm_up("warm_second", nc.vector.tensor_copy, AT_THIRD, (2, 3))
         finish_table("v", v_codes, v_scales, v_bf, v_late[1][:])
 
         xm_codes = [placed("xm_codes0", [P, P], U32, AT_H), sb("xm_codes1", [P, P], U32)]

from contextlib import ExitStack

import concourse.mybir as mybir

N, T, D, R = 512, 2048, 512, 512
FLOPS = 3 * 2 * D * R * N

F32 = mybir.dt.float32
BF16 = mybir.dt.bfloat16
U32 = mybir.dt.uint32
U16 = mybir.dt.uint16
U8 = mybir.dt.uint8
E4M3 = mybir.dt.float8_e4m3fn_x4
E5M2 = mybir.dt.float8_e5m2_x4
ALU = mybir.AluOpType
ACT = mybir.ActivationFunctionType

P = 128
PACK = 4
QUARTERS = 4
Q = N // QUARTERS
HALF = N // 2
PER_COLUMN = 16
BLOCKS = D // P
WARM_ROWS = 32
ALIGN = 256
KIB = 1024


def tile_attend_ghv_lch_kernel(tc, xT, wT, vT, y, wt, xm, offs, out):
    nc = tc.nc
    with ExitStack() as ctx:
        keep = ctx.enter_context(tc.tile_pool(name="keep", bufs=1))
        shared = ctx.enter_context(tc.tile_pool(name="shared", bufs=1))
        psum = ctx.enter_context(tc.psum_pool(name="psum", bufs=1))

        def sb(name, shape, dtype):
            return keep.tile(shape, dtype, name=name, align_bytes=ALIGN)

        def placed(name, shape, dtype, offset):
            return shared.tile(shape, dtype, name=name, align_bytes=ALIGN, offset=offset)

        AT_Q2, AT_ZEROS, AT_DENSE, AT_WBF, AT_VBF, AT_H, AT_THIRD = [KIB * k for k in (0, 5, 6, 8, 10, 12, 14)]

        quarter = [slice(n * Q, (n + 1) * Q) for n in range(QUARTERS)]
        half = [slice(0, HALF), slice(HALF, N)]
        block = [slice(m * P, (m + 1) * P) for m in range(BLOCKS)]

        offsets = keep.tile([P, N // PER_COLUMN], U16, name="offsets", align_bytes=ALIGN)

        def listed(slots):
            return offsets[:, slots.start // PER_COLUMN : slots.stop // PER_COLUMN]

        x_raw = sb("x_raw", [P, PACK, R], F32)
        w_pair = sb("w_pair", [P, 2, T], F32)
        w_late = [sb(f"w_late{u}", [P, T], F32) for u in range(2)]
        v_pair = sb("v_pair", [P, 2, T], F32)
        v_late = [placed("v_late0", [P, T], F32, AT_THIRD), sb("v_late1", [P, T], F32)]
        y_sb = sb("y_sb", [P, PACK, N], F32)
        wt_sb = sb("wt_sb", [P, PACK], F32)
        xm_first = sb("xm_first", [P, PACK, P], F32)
        xm_rest = sb("xm_rest", [P, PACK, D - P], F32)
        xm_block = [xm_first[:]] + [xm_rest[:, :, block[m]] for m in range(BLOCKS - 1)]

        def load_table(table, pair, late):
            rows = table.rearrange("(p t) c -> p t c", t=PACK)
            nc.sync.dma_start(out=pair[:], in_=rows[:, 0:2, :])
            for u in range(2):
                nc.sync.dma_start(out=late[u][:], in_=rows[:, 2 + u, :])

        nc.scalar.dma_start(out=wt_sb[:], in_=wt.rearrange("b (p t) o -> p (b t o)", t=PACK))
        nc.sync.dma_start(out=x_raw[:], in_=xT.rearrange("b (p t) r -> p (b t) r", t=PACK))
        nc.sync.dma_start(offsets[:], offs)
        load_table(wT, w_pair, w_late)
        nc.sync.dma_start(out=y_sb[:], in_=y.rearrange("b (p t) i -> p (b t) i", t=PACK))
        load_table(vT, v_pair, v_late)
        xm_rows = xm.rearrange("b (p t) d -> p (b t) d", t=PACK)
        nc.sync.dma_start(out=xm_first[:], in_=xm_rows[:, :, 0:P])
        nc.sync.dma_start(out=xm_rest[:], in_=xm_rows[:, :, P:D])

        wide = [sb(f"wide{m}", [P, T], F32) for m in range(BLOCKS)]
        for m in range(BLOCKS):
            nc.vector.memset(wide[m][:].bitcast(U32), 0)
        zeros = placed("zeros", [P, Q], F32, AT_ZEROS)
        nc.vector.memset(zeros[:], 0.0)

        x_bf = sb("x_bf", [P, R * PACK], BF16)
        x_codes = sb("x_codes", [P, R], U32)
        x_scales = sb("x_scales", [P, R], U8)
        nc.scalar.copy(
            out=x_bf[:].rearrange("p (t m j) -> p m t j", t=PACK, j=PACK),
            in_=x_raw[:].rearrange("p j (m t) -> p m t j", t=PACK),
        )
        nc.vector.quantize_mx(out=x_codes[:].bitcast(E4M3), scales=x_scales[:], in_=x_bf[:])

        def scores(bank_name, codes, scales, n):
            bank = psum.tile([P, PACK, Q], F32, name=bank_name)
            for t in range(PACK):
                nc.tensor.matmul_mx(
                    out=bank[:, t, :],
                    lhsT=x_codes[:, block[t]].bitcast(E4M3),
                    lhsT_scale=x_scales[:, block[t]],
                    rhs=codes[n][:].bitcast(E4M3),
                    rhs_scale=scales[:, quarter[n]],
                    start=True,
                    stop=True,
                )
            return bank

        def gather_on_vector(dst, plane, slots):
            nc.vector.tensor_copy(dst, plane.indirect(listed(slots)))

        def gather_on_scalar(dst, plane, slots):
            nc.scalar.activation(out=dst, in_=plane.indirect(listed(slots)), func=ACT.Copy)

        def rounded(name, at):
            bf = [placed(f"{name}0", [P, Q, PACK], BF16, at)]
            return bf + [sb(f"{name}{n}", [P, Q, PACK], BF16) for n in range(1, QUARTERS)]

        def coded(name, at):
            codes = [sb(f"{name}_codes{n}", [P, Q], U32) for n in (0, 1, 3)]
            return codes[0:2] + [placed(f"{name}_codes2", [P, Q], U32, at), codes[2]], sb(f"{name}_scales", [P, N], U8)

        def gather_front(front, plane, t):
            gather_on_scalar(front[0][:, t, :], plane, half[0])
            gather_on_vector(front[1][:, t, :], plane, half[1])

        def place_front(bf, front, n):
            copy = nc.scalar.copy if n == 0 else nc.vector.tensor_copy
            copy(out=bf[n][:, :, 0:2], in_=front[n // 2][:, :, quarter[n % 2]].rearrange("p t c -> p c t"))

        def gather_back(bf, staged, plane, t):
            for n in (0, 1, 3):
                gather_on_scalar(bf[n][:, :, t], plane, quarter[n])
            gather_on_vector(staged[:], plane, quarter[2])

        def place_back(bf, staged, t):
            nc.vector.tensor_copy(out=bf[2][:, :, t], in_=staged[:])

        def quantize_table(codes, scales, bf, n):
            nc.vector.quantize_mx(
                out=codes[n][:].bitcast(E4M3),
                scales=scales[:, quarter[n]],
                in_=bf[n][:].rearrange("p c t -> p (c t)"),
            )

        def finish_table(name, codes, scales, bf, plane):
            last = [sb(f"{name}_last{n}", [P, Q], F32) for n in range(2)]
            for n in range(2):
                gather_on_scalar(bf[n][:, :, 3], plane, quarter[n])
                gather_on_vector(last[n][:], plane, quarter[2 + n])
            nc.scalar.copy(out=bf[3][:, :, 3], in_=last[1][:])
            place_back(bf, last[0], 3)
            for n in range(QUARTERS):
                quantize_table(codes, scales, bf, n)

        w_front = [sb(f"w_front{u}", [P, 2, HALF], F32) for u in range(2)]
        w_third = sb("w_third", [P, Q], F32)
        w_bf = rounded("w_bf", AT_WBF)
        w_codes, w_scales = coded("w", AT_WBF)
        for t in range(2):
            gather_front(w_front, w_pair[:, t, :], t)
        for n in range(QUARTERS):
            place_front(w_bf, w_front, n)
        gather_back(w_bf, w_third, w_late[0][:], 2)
        place_back(w_bf, w_third, 2)
        finish_table("w", w_codes, w_scales, w_bf, w_late[1][:])

        z = sb("z", [P, N, PACK], F32)
        q = sb("q", [P, N, PACK], F32)
        q2 = [sb(f"q2_{n}", [P, Q, PACK], F32) for n in range(QUARTERS - 1)]
        q2.append(placed("q2_3", [P, Q, PACK], F32, AT_Q2))
        h = [placed("h0", [P, Q, PACK], F32, AT_H)]
        h.extend(sb(f"h{n}", [P, Q, PACK], F32) for n in range(1, QUARTERS))

        def square(n):
            if n == 0:
                nc.vector.tensor_tensor(out=q2[n][:], in0=q[:, quarter[n], :], in1=q[:, quarter[n], :], op=ALU.mult)
            else:
                nc.scalar.activation(out=q2[n][:], in_=q[:, quarter[n], :], func=ACT.Square)

        for n in range(QUARTERS):
            a = scores(f"bank{n}", w_codes, w_scales, n)
            nc.vector.tensor_tensor(
                out=z[:, quarter[n], :].rearrange("p (c i) t -> p c t i", i=4),
                in0=a[:].rearrange("p t (c i) -> p c t i", i=4),
                in1=y_sb[:, :, quarter[n]].rearrange("p t (c i) -> p c t i", i=4),
                op=ALU.subtract,
            )
            nc.scalar.activation(out=q[:, quarter[n], :], in_=z[:, quarter[n], :], func=ACT.Tanh)
        for n in range(QUARTERS):
            square(n)

        neg_wt = sb("neg_wt", [P, PACK], F32)
        nc.vector.tensor_scalar(out=neg_wt[:], in0=wt_sb[:], scalar1=-1.0, scalar2=None, op0=ALU.mult)

        def form_h(n):
            nc.vector.scalar_tensor_tensor(
                out=h[n][:],
                in0=q2[n][:],
                scalar=1.0,
                in1=neg_wt[:].unsqueeze(1).to_broadcast([P, Q, PACK]),
                op0=ALU.subtract,
                op1=ALU.mult,
            )

        def warm_up(name, copy, offset, banks):
            codes = placed(name, [P, WARM_ROWS], U32, offset)
            copy(out=codes[:], in_=w_codes[0][:, 0:WARM_ROWS])
            for n in banks:
                bank = psum.tile([P, N], F32, name=f"bank{n}")
                nc.tensor.matmul_mx(
                    out=bank[0:WARM_ROWS, :],
                    lhsT=codes[:].bitcast(E4M3),
                    lhsT_scale=w_scales[:, 0:WARM_ROWS],
                    rhs=x_codes[:].bitcast(E4M3),
                    rhs_scale=x_scales[:],
                    start=True,
                    stop=True,
                )

        v_front = [sb(f"v_front{u}", [P, 2, HALF], F32) for u in range(2)]
        v_third = sb("v_third", [P, Q], F32)
        v_bf = rounded("v_bf", AT_VBF)
        v_codes, v_scales = coded("v", AT_VBF)
        for n in range(QUARTERS):
            form_h(n)
        for t in range(2):
            gather_front(v_front, v_pair[:, t, :], t)
        place_front(v_bf, v_front, 0)
        warm_up("warm_first", nc.scalar.copy, AT_Q2, (0, 1))
        for n in range(1, QUARTERS):
            place_front(v_bf, v_front, n)
        gather_back(v_bf, v_third, v_late[0][:], 2)
        place_back(v_bf, v_third, 2)
        warm_up("warm_second", nc.vector.tensor_copy, AT_THIRD, (2, 3))
        finish_table("v", v_codes, v_scales, v_bf, v_late[1][:])

        xm_codes = [placed("xm_codes0", [P, P], U32, AT_H), sb("xm_codes1", [P, P], U32)]
        xm_codes.append(placed("xm_codes2", [P, P], U32, AT_ZEROS - P * 2))
        xm_codes.append(placed("xm_codes3", [P, P], U32, AT_ZEROS + P * 2))
        xm_scales = sb("xm_scales", [P, D], U8)
        xm_bf = [sb(f"xm_bf{m}", [P, P, PACK], BF16) for m in range(BLOCKS - 1)]
        xm_bf.append(placed("xm_bf3", [P, P, PACK], BF16, AT_DENSE))

        def round_xm(m):
            nc.scalar.copy(
                out=xm_bf[m][:].rearrange("p (c i) t -> p c t i", i=4),
                in_=xm_block[m].rearrange("p t (c i) -> p c t i", i=4),
            )

        def quantize_xm(m):
            nc.vector.quantize_mx(
                out=xm_codes[m][:].bitcast(E4M3),
                scales=xm_scales[:, block[m]],
                in_=xm_bf[m][:].rearrange("p c t -> p (c t)"),
            )

        for m in range(BLOCKS - 1):
            round_xm(m)

        g_bf = sb("g_bf", [P, N, PACK], BF16)
        g_codes = sb("g_codes", [P, N], U32)
        g_scales = sb("g_scales", [P, N], U8)
        av = [scores(f"bank{QUARTERS + n}", v_codes, v_scales, n) for n in range(QUARTERS)]

        def form_g(slots):
            n = slots.start // Q
            own = slice(slots.start - n * Q, slots.stop - n * Q)
            nc.vector.tensor_tensor(
                out=g_bf[:, slots, :],
                in0=av[n][:, :, own].rearrange("p t i -> p i t"),
                in1=h[n][:, own, :],
                op=ALU.mult,
            )

        def quantize_g(slots):
            nc.vector.quantize_mx(
                out=g_codes[:, slots].bitcast(E5M2),
                scales=g_scales[:, slots],
                in_=g_bf[:, slots, :].rearrange("p i t -> p (i t)"),
            )

        dense = [placed("dense0", [P, N], F32, AT_DENSE)]
        dense.extend(sb(f"dense{m}", [P, N], F32) for m in range(1, BLOCKS))

        def product(bank_name, m, slots):
            dw = psum.tile([P, slots.stop - slots.start], F32, name=bank_name)
            nc.tensor.matmul_mx(
                out=dw[:],
                lhsT=xm_codes[m][:].bitcast(E4M3),
                lhsT_scale=xm_scales[:, block[m]],
                rhs=g_codes[:, slots].bitcast(E5M2),
                rhs_scale=g_scales[:, slots],
                start=True,
                stop=True,
            )
            nc.scalar.copy(out=dense[m][:, slots], in_=dw[:])

        eighths = [slice(N - Q, N - Q // 2), slice(N - Q // 2, N)]
        form_g(quarter[0])
        form_g(quarter[1])
        quantize_xm(0)
        form_g(quarter[2])
        quantize_g(half[0])
        product("bank0", 0, half[0])
        quantize_g(quarter[2])
        product("bank1", 0, quarter[2])
        for slots in eighths:
            form_g(slots)
        quantize_g(eighths[0])
        quantize_xm(1)
        quantize_g(eighths[1])
        product("bank2", 0, quarter[3])
        early = slice(0, N - Q)
        nc.vector.tensor_copy(wide[0][:].indirect(listed(early)), dense[0][:, early])
        nc.vector.tensor_tensor(
            out=wide[0][:].indirect(listed(quarter[3])),
            in0=dense[0][:, quarter[3]],
            in1=zeros[:],
            op=ALU.add,
        )
        nc.sync.dma_start(out=out[block[0], :], in_=wide[0][:])

        def finish(m):
            product(f"bank{(m + 2) % QUARTERS}", m, slice(0, N))
            nc.vector.tensor_copy(wide[m][:].indirect(offsets[:]), dense[m][:])
            nc.sync.dma_start(out=out[block[m], :], in_=wide[m][:])

        quantize_xm(2)
        finish(1)
        round_xm(3)
        quantize_xm(3)
        finish(2)
        finish(3)
